import numpy as np
import ml_dtypes


def mxq(x, axis, fmt="e4m3"):
    dtype, down = {"e4m3": (ml_dtypes.float8_e4m3fn, 7), "e5m2": (ml_dtypes.float8_e5m2, 14)}[fmt]
    v = np.moveaxis(np.asarray(x, np.float32).astype(ml_dtypes.bfloat16).astype(np.float64), axis, -1)
    blocks = v.reshape(v.shape[:-1] + (-1, 32))
    amax = np.abs(blocks).max(-1, keepdims=True)
    byte = np.maximum(np.where(amax > 0, np.frexp(amax)[1] - 1 + 127, 0) - down, 1)
    scale = np.exp2(byte - 127.0)
    codes = (blocks / scale).astype(np.float32).astype(dtype).astype(np.float64)
    return np.moveaxis((codes * scale).reshape(v.shape), -1, axis)


WIDE = False


def mx_kscale(k):
    if not WIDE:
        return np.ones(k)
    levels = np.array([10, -10, 5, -5, 0])
    if k % 512:
        return np.exp2(np.random.permutation(np.resize(levels, k // 32))).repeat(32)
    a = np.empty((k // 512, 16))
    for p in range(k // 512):
        a[p, :8] = np.random.permutation(np.resize(levels, 8))
        for g in range(8):
            far = levels[np.abs(levels - a[p, g]) >= 10]
            a[p, g + 8] = far[np.random.randint(len(far))]
    return np.exp2(a.ravel()).repeat(32)


BF16 = ml_dtypes.bfloat16


def bf(x):
    return np.asarray(x, np.float32).astype(BF16)


def f64(x):
    return np.asarray(x).astype(np.float64)


E2M1 = np.array([0.0, 0.5, 1.0, 1.5, 2.0, 3.0, 4.0, 6.0, -0.0, -0.5, -1.0, -1.5, -2.0, -3.0, -4.0, -6.0])


def pack_weight(w, fmt):
    k, n = w.shape
    w = f64(bf(w)).reshape(k // 32, 32, n)
    amax = np.abs(w).max(1)
    if fmt == "e4m3":
        byte = np.frexp(amax)[1] - 1 + 127 - 7
    else:
        mant, ex = np.frexp(amax / 6.0)
        byte = np.where(mant > 0.5, ex, ex - 1) + 127
    byte = np.clip(np.where(amax > 0, byte, 1), 1, 254)
    scaled = (w * np.exp2(127.0 - byte)[:, None, :]).reshape(k, n).astype(np.float32)
    by_word = np.ascontiguousarray(scaled.reshape(k // 512, 128, 4, n).transpose(0, 1, 3, 2))
    if fmt == "e4m3":
        words = by_word.astype(ml_dtypes.float8_e4m3fn).view(np.uint8)
    else:
        c = by_word.astype(ml_dtypes.float4_e2m1fn).view(np.uint8) & 0xF
        words = c[..., 0::2] | (c[..., 1::2] << 4)
    return np.ascontiguousarray(words), np.ascontiguousarray(byte.astype(np.uint8).reshape(k // 512, 16, n))


def unpack_weight(words, scales, fmt):
    g, p, n, _ = words.shape
    if fmt == "e4m3":
        vals = np.ascontiguousarray(words).view(ml_dtypes.float8_e4m3fn).astype(np.float64)
    else:
        nib = np.empty((g, p, n, 4), np.uint8)
        nib[..., 0::2] = words & 0xF
        nib[..., 1::2] = words >> 4
        vals = E2M1[nib]
    vals = vals * np.repeat(np.exp2(scales.astype(np.float64) - 127.0), 8, axis=1)[..., None]
    return vals.transpose(0, 1, 3, 2).reshape(g * 512, n)
def pack4(w):
    words, scales = pack_weight(w, "e2m1")
    return words.reshape(words.shape[0], 128, -1), scales


def unpack4(words, scales):
    return unpack_weight(words.reshape(words.shape[0], 128, -1, 2), scales, "e2m1")


def planes(Y):
    n, m = Y.shape
    b = f64(bf(Y)).reshape(n // 32, 32, m)
    amax = np.abs(b).max(1)
    byte = np.clip(np.where(amax > 0, np.frexp(amax)[1] - 1 + 127 - 7, 1), 1, 254)
    codes = (b * np.exp2(127.0 - byte)[:, None, :]).reshape(n, m).astype(np.float32).astype(ml_dtypes.float8_e4m3fn).view(np.uint8)
    words = codes.reshape(n // 512, 128, 4, m).transpose(0, 1, 3, 2)
    return np.ascontiguousarray(words), np.ascontiguousarray(byte.astype(np.uint8).reshape(n // 512, 16, m))


M, K, R, N = 1024, 1536, 512, 2048

def setup_inputs():
    s = mx_kscale(K)
    t = mx_kscale(R)
    x = bf(np.random.randn(M, K) * s)
    w_words, w_scales = pack4(np.random.randn(K, N) / np.sqrt(K) / s[:, None])
    chan = bf(np.exp(0.3 * np.random.randn(N)))
    z = bf(np.random.randn(M, R))
    lam = bf(np.exp(0.5 * np.random.randn(R)) * t)
    u = bf(0.6 * np.random.randn(R, N) / np.sqrt(R) / t[:, None])
    up = bf(np.random.randn(M, N) * np.exp(0.8 * np.random.randn(N)))
    return {"x": x, "w_words": w_words, "w_scales": w_scales, "chan": chan,
            "z": z, "lam": lam, "u": u, "up": up}

def reference(x, w_words, w_scales, chan, z, lam, u, up):
    w = unpack4(w_words, w_scales)
    base = mxq(f64(x), 1, "e4m3") @ w
    zl = f64(z) * f64(lam)
    corr = mxq(zl, 1, "e4m3") @ mxq(f64(u), 0, "e4m3")
    gate = base * f64(chan) + corr
    y = gate / (1.0 + np.exp(-gate)) * f64(up)
    Y = y.reshape(M, N).T
    words, scales = planes(Y)
    return y, words, scales

@@ -1,0 +1,406 @@
+from contextlib import ExitStack
+
+import concourse.mybir as mybir
+from concourse.masks import make_identity
+
+M, K, R, N = 1024, 1536, 512, 2048
+FLOPS = 2 * M * N * (K + R)
+
+F32 = mybir.dt.float32
+BF16 = mybir.dt.bfloat16
+I32 = mybir.dt.int32
+U32 = mybir.dt.uint32
+U8 = mybir.dt.uint8
+FP8X4 = mybir.dt.float8_e4m3fn_x4
+FP4X4 = mybir.dt.float4_e2m1fn_x4
+MULT = mybir.AluOpType.mult
+ADD = mybir.AluOpType.add
+SILU = mybir.ActivationFunctionType.Silu
+
+P = 128
+PASS = 512
+TILES = M // P
+GROUPS = N // PASS
+X_PASSES = K // PASS
+STEPS = [(m, g) for g in range(GROUPS) for m in range(2)] + [(m, g) for m in range(2, TILES) for g in range(GROUPS)]
+LAST = len(STEPS) - 1
+U_SPLIT = 256
+Y_BUFS = 20
+EARLY_SCALE_TILES = 6
+
+
+def tile_frozen_fp4_lowrank_gate_g5_kernel(tc, x, w_words, w_scales, chan, z, lam, u, up, out_0, out_1, out_2):
+    nc = tc.nc
+    with ExitStack() as ctx:
+        sb = ctx.enter_context(tc.tile_pool(name="sb", bufs=1))
+        ps = ctx.enter_context(tc.psum_pool(name="ps", bufs=2))
+        ctx.enter_context(tc.manual_schedule())
+
+        x_raw, z_raw, up_raw, u_raw, w_codes = {}, {}, {}, {}, {}
+        act_codes, act_scales, u_codes, u_scales, u_grouped = {}, {}, {}, {}, {}
+        bank_a, bank_b, x_grouped_a, x_grouped_b, z_grouped = {}, {}, {}, {}, {}
+        base, corr, y, y_sorted, y_bank, y_grouped = {}, {}, {}, {}, {}, {}
+
+        def load_x(m):
+            x_raw[m] = sb.tile([P, K], BF16, name="x_raw", bufs=TILES, align_bytes=64)
+            nc.sync.dma_start(out=x_raw[m][:], in_=x[m * P:(m + 1) * P, :])
+
+        def load_z(m):
+            z_raw[m] = sb.tile([P, R], BF16, name="z_raw", bufs=TILES, align_bytes=64)
+            nc.sync.dma_start(out=z_raw[m][:], in_=z[m * P:(m + 1) * P, :])
+
+        def load_up(m, half):
+            up_raw[m, half] = sb.tile([P, N // 2], BF16, name="up_raw", bufs=2 * TILES, align_bytes=64)
+            nc.sync.dma_start(out=up_raw[m, half][:], in_=up[m * P:(m + 1) * P, half * (N // 2):(half + 1) * (N // 2)])
+
+        def load_u(g):
+            u_raw[g] = sb.tile([P, 4, PASS], BF16, name="u_raw", bufs=GROUPS, align_bytes=64)
+            nc.sync.dma_start(out=u_raw[g][:], in_=u[:, g * PASS:(g + 1) * PASS].rearrange("(p t) n -> p t n", t=4))
+
+        def load_w(g):
+            w_codes[g] = sb.tile([P, X_PASSES, 2 * PASS], U8, name="w_codes", bufs=GROUPS, align_bytes=64)
+            nc.sync.dma_start(
+                out=w_codes[g][:].bitcast(I32),
+                in_=w_words.rearrange("k p b -> p k b")[:, :, g * 2 * PASS:(g + 1) * 2 * PASS].bitcast(I32),
+            )
+
+        ident = sb.tile([P, P], F32, name="ident", align_bytes=64)
+        make_identity(nc, ident[:])
+        w_plane = sb.tile([P, X_PASSES, N], U8, name="w_plane", align_bytes=64)
+        nc.vector.memset(w_plane[:].bitcast(I32), 0)
+        chan_rows = sb.tile([P, N // P], BF16, name="chan_rows", align_bytes=64)
+        lam_rows = sb.tile([P, 4], BF16, name="lam_rows", align_bytes=64)
+        chan_all = sb.tile([P, N], BF16, name="chan_all", align_bytes=64)
+
+        load_x(0)
+        load_u(0)
+        nc.sync.dma_start(out=chan_rows[:], in_=chan.rearrange("(p c) -> p c", p=P))
+        for q in range(4):
+            nc.sync.dma_start(
+                out=w_plane[32 * q:32 * q + 4, :, :].bitcast(I32),
+                in_=w_scales[:, 4 * q:4 * q + 4, :].rearrange("k r n -> r k n").bitcast(I32),
+            )
+        load_z(0)
+        nc.sync.dma_start(out=lam_rows[:], in_=lam.rearrange("(p t) -> p t", t=4))
+        load_w(0)
+        load_x(1)
+        load_z(1)
+        load_w(1)
+        load_up(0, 0)
+        load_u(1)
+        load_up(1, 0)
+        load_w(2)
+        load_u(2)
+        load_w(3)
+        load_x(2)
+        load_u(3)
+        load_z(2)
+        load_up(0, 1)
+        load_up(1, 1)
+        for m in range(2, TILES):
+            if m > 2:
+                load_x(m)
+                load_z(m)
+            load_up(m, 0)
+            load_up(m, 1)
+
+        word_stores = [(0, 2, 0, 4), (2, 4, 0, 4), (4, 6, 0, 4), (6, 7, 0, 4), (7, 8, 0, 2), (7, 8, 2, 4)]
+        out_words = {}
+        for part in word_stores:
+            m0, m1, g0, g1 = part
+            out_words[part] = sb.tile([P, g1 - g0, (m1 - m0) * P], U32, name="out_words_%d_%d" % (m0, g0), align_bytes=64)
+        scale_stores = [(0, EARLY_SCALE_TILES), (EARLY_SCALE_TILES, TILES)]
+        out_scales = {}
+        for part in scale_stores:
+            out_scales[part] = sb.tile([P, GROUPS, (part[1] - part[0]) * P], U8, name="out_scales_%d" % part[0], align_bytes=64)
+        quantised = set()
+
+        def new_bank():
+            return ps.tile([P, 4, P], F32, name="turn_bank", bufs=4)
+
+        def turn_words(bank, slot, words):
+            for h in range(2):
+                nc.tensor.transpose(bank[:, slot + h, :], words[:, h:2 * P:2], ident[:])
+
+        def turn_a(m):
+            bank_a[m] = new_bank()
+            words = x_raw[m][:].bitcast(F32)
+            turn_words(bank_a[m], 0, words[:, 0:2 * P])
+            turn_words(bank_a[m], 2, words[:, 2 * P:4 * P])
+
+        def turn_b(m):
+            bank_b[m] = new_bank()
+            turn_words(bank_b[m], 0, x_raw[m][:].bitcast(F32)[:, 4 * P:6 * P])
+            turn_words(bank_b[m], 2, z_raw[m][:].bitcast(F32))
+
+        def group_a(m):
+            x_grouped_a[m] = sb.tile([P, 2 * PASS], BF16, name="x_grouped_a", bufs=2, align_bytes=64)
+            nc.scalar.copy(
+                out=x_grouped_a[m][:].bitcast(F32).rearrange("p (k r h) -> p k r h", k=2, h=2),
+                in_=bank_a[m][:].rearrange("p (k h) r -> p k r h", h=2),
+            )
+
+        def group_b(m):
+            x_grouped_b[m] = sb.tile([P, PASS], BF16, name="x_grouped_b", bufs=2, align_bytes=64)
+            nc.scalar.copy(
+                out=x_grouped_b[m][:].bitcast(F32).rearrange("p (r h) -> p r h", h=2),
+                in_=bank_b[m][:, 0:2, :].rearrange("p h r -> p r h"),
+            )
+
+        def scale_z(m):
+            z_grouped[m] = sb.tile([P, PASS], BF16, name="z_grouped", bufs=2, align_bytes=64)
+            nc.vector.tensor_tensor(
+                out=z_grouped[m][:].rearrange("p (r h e) -> p r h e", h=2, e=2),
+                in0=bank_b[m][:, 2:4, :].bitcast(BF16).rearrange("p h (r e) -> p r h e", e=2),
+                in1=lam_rows[:].rearrange("p (h e) -> p h e", e=2).unsqueeze(1).to_broadcast([P, P, 2, 2]),
+                op=MULT,
+            )
+
+        def quantise(codes, scales, values):
+            nc.vector.quantize_mx(out=codes.bitcast(FP8X4), scales=scales, in_=values)
+
+        def quantise_a(m):
+            act_codes[m] = sb.tile([P, 4 * P], U32, name="act_codes", bufs=3, align_bytes=64)
+            act_scales[m] = sb.tile([P, 4 * P], U8, name="act_scales", bufs=3, align_bytes=64)
+            quantise(act_codes[m][:, 0:2 * P], act_scales[m][:, 0:2 * P], x_grouped_a[m][:])
+
+        def quantise_b(m):
+            quantise(act_codes[m][:, 2 * P:3 * P], act_scales[m][:, 2 * P:3 * P], x_grouped_b[m][:])
+
+        def quantise_z(m):
+            quantise(act_codes[m][:, 3 * P:4 * P], act_scales[m][:, 3 * P:4 * P], z_grouped[m][:])
+
+        def u_views(g, c0, c1):
+            dst = u_grouped[g][:].rearrange("p (n t) -> p n t", t=4)[:, c0:c1, :]
+            return dst.rearrange("p (c i) t -> p c t i", i=4), u_raw[g][:, :, c0:c1].rearrange("p t (c i) -> p c t i", i=4)
+
+        def group_u_vector(g):
+            u_grouped[g] = sb.tile([P, 4 * PASS], BF16, name="u_grouped", bufs=2, align_bytes=64)
+            dst, src = u_views(g, 0, U_SPLIT)
+            nc.vector.tensor_copy(out=dst, in_=src)
+
+        def group_u_scalar(g):
+            dst, src = u_views(g, U_SPLIT, PASS)
+            nc.scalar.copy(out=dst, in_=src)
+
+        def quantise_u(g):
+            u_codes[g] = sb.tile([P, PASS], U32, name="u_codes", bufs=GROUPS, align_bytes=64)
+            u_scales[g] = sb.tile([P, PASS], U8, name="u_scales", bufs=GROUPS, align_bytes=64)
+            quantise(u_codes[g][:], u_scales[g][:], u_grouped[g][:])
+
+        def spread_chan():
+            words = chan_rows[:].bitcast(F32)
+            banks = []
+            for b in range(2):
+                bank = new_bank()
+                for j in range(4):
+                    c = 4 * b + j
+                    nc.tensor.transpose(bank[:, j, :], words[:, c:c + 1].to_broadcast([P, P]), ident[:])
+                banks.append(bank)
+            return banks
+
+        def copy_chan(banks):
+            dst = chan_all[:].bitcast(F32).rearrange("q (p c) -> q p c", p=P)
+            for b in range(2):
+                nc.scalar.copy(out=dst[:, :, 4 * b:4 * b + 4], in_=banks[b][:].rearrange("q j p -> q p j"))
+
+        def base_matmul(s):
+            m, g = STEPS[s]
+            base[s] = ps.tile([P, PASS], F32, name="base")
+            for k in range(X_PASSES):
+                nc.tensor.matmul_mx(
+                    out=base[s][:],
+                    lhsT=act_codes[m][:, k * P:(k + 1) * P].bitcast(FP8X4),
+                    lhsT_scale=act_scales[m][:, k * P:(k + 1) * P],
+                    rhs=w_codes[g][:, k, :].bitcast(FP4X4),
+                    rhs_scale=w_plane[:, k, g * PASS:(g + 1) * PASS],
+                    start=(k == 0),
+                    stop=(k == X_PASSES - 1),
+                )
+
+        def corr_matmul(s):
+            m, g = STEPS[s]
+            corr[s] = ps.tile([P, PASS], F32, name="corr")
+            nc.tensor.matmul_mx(
+                out=corr[s][:],
+                lhsT=act_codes[m][:, 3 * P:4 * P].bitcast(FP8X4),
+                lhsT_scale=act_scales[m][:, 3 * P:4 * P],
+                rhs=u_codes[g][:].bitcast(FP8X4),
+                rhs_scale=u_scales[g][:],
+                start=True,
+                stop=True,
+            )
+
+        def times_chan(s):
+            g = STEPS[s][1]
+            y[s] = sb.tile([P, PASS], F32, name="y", bufs=Y_BUFS, align_bytes=64)
+            nc.vector.tensor_tensor(out=y[s][:], in0=base[s][:], in1=chan_all[:, g * PASS:(g + 1) * PASS], op=MULT)
+
+        def plus_corr(s):
+            nc.vector.tensor_tensor(out=y[s][:], in0=corr[s][:], in1=y[s][:], op=ADD)
+
+        def silu(s):
+            nc.scalar.activation(out=y[s][:], in_=y[s][:], func=SILU)
+
+        def times_up(s, engine):
+            m, g = STEPS[s]
+            cols = slice((g % 2) * PASS, (g % 2 + 1) * PASS)
+            engine.tensor_tensor(out=y[s][:], in0=y[s][:], in1=up_raw[m, g // 2][:, cols], op=MULT)
+
+        def store_y(s):
+            m, g = STEPS[s]
+            nc.sync.dma_start(out=out_0[m * P:(m + 1) * P, g * PASS:(g + 1) * PASS], in_=y[s][:])
+
+        def round_views(s):
+            y_sorted[s] = sb.tile([P, PASS], BF16, name="y_sorted", bufs=4, align_bytes=64)
+            return (y_sorted[s][:].rearrange("r (h p e) -> r h p e", h=2, e=2),
+                    y[s][:].rearrange("r (p h e) -> r h p e", h=2, e=2))
+
+        def round_y(s):
+            dst, src = round_views(s)
+            nc.scalar.copy(out=dst, in_=src)
+
+        def turn_y(steps):
+            y_bank[steps] = new_bank()
+            for j, s in enumerate(steps):
+                words = y_sorted[s][:].bitcast(F32)
+                for h in range(2):
+                    nc.tensor.transpose(y_bank[steps][:, 2 * j + h, :], words[:, h * P:(h + 1) * P], ident[:])
+
+        def group_y_views(steps):
+            n = len(steps)
+            y_grouped[steps] = sb.tile([P, 2 * PASS], BF16, name="y_grouped", bufs=3, align_bytes=64)
+            return (y_grouped[steps][:, 0:n * PASS].bitcast(F32).rearrange("p (j r h) -> p j r h", j=n, h=2),
+                    y_bank[steps][:, 0:2 * n, :].rearrange("p (j h) r -> p j r h", h=2))
+
+        def group_y(steps):
+            dst, src = group_y_views(steps)
+            nc.scalar.copy(out=dst, in_=src)
+
+        def quantise_y(steps):
+            for j, s in enumerate(steps):
+                m, g = STEPS[s]
+                wpart = [t for t in word_stores if t[0] <= m < t[1] and t[2] <= g < t[3]][0]
+                spart = [t for t in scale_stores if t[0] <= m < t[1]][0]
+                wcol = (m - wpart[0]) * P
+                scol = (m - spart[0]) * P
+                quantise(out_words[wpart][:, g - wpart[2], wcol:wcol + P],
+                         out_scales[spart][:, g, scol:scol + P],
+                         y_grouped[steps][:, j * PASS:(j + 1) * PASS])
+                quantised.add((m, g))
+                m0, m1, g0, g1 = wpart
+                if all((a, b) in quantised for a in range(m0, m1) for b in range(g0, g1)):
+                    nc.sync.dma_start(
+                        out=out_1[g0:g1].rearrange("g p m t -> p g (m t)")[:, :, m0 * P * 4:m1 * P * 4].bitcast(I32),
+                        in_=out_words[wpart][:].bitcast(I32),
+                    )
+                m0, m1 = spart
+                if all((a, b) in quantised for a in range(m0, m1) for b in range(GROUPS)):
+                    for q in range(4):
+                        queue = nc.scalar if (m1 == TILES and q >= 2) else nc.sync
+                        queue.dma_start(
+                            out=out_2[:, 4 * q:4 * q + 4, m0 * P:m1 * P].rearrange("g r m -> r g m").bitcast(I32),
+                            in_=out_scales[spart][32 * q:32 * q + 4, :, :].bitcast(I32),
+                        )
+
+        turn_a(0)
+        chan_banks = spread_chan()
+        turn_b(0)
+        group_a(0)
+        group_u_vector(0)
+        group_u_scalar(0)
+        quantise_a(0)
+        scale_z(0)
+        group_b(0)
+        copy_chan(chan_banks)
+        quantise_u(0)
+        quantise_b(0)
+        quantise_z(0)
+        base_matmul(0)
+        corr_matmul(0)
+        turn_a(1)
+        turn_b(1)
+        times_chan(0)
+        group_a(1)
+        plus_corr(0)
+        quantise_a(1)
+        group_b(1)
+        silu(0)
+        times_up(0, nc.gpsimd)
+        quantise_b(1)
+        scale_z(1)
+        base_matmul(1)
+        base_matmul(2)
+        times_chan(1)
+        quantise_z(1)
+        corr_matmul(1)
+        group_u_vector(1)
+        group_u_scalar(1)
+
+        def matmuls(s):
+            if s + 2 <= LAST:
+                base_matmul(s + 2)
+            if s + 1 <= LAST:
+                corr_matmul(s + 1)
+
+        for s in range(1, LAST):
+            even = s % 2 == 0
+            nxt_a = (s + 6) // 4 if (s + 6) % 4 == 0 and (s + 6) // 4 in range(2, TILES) else None
+            nxt_b = (s + 4) // 4 if (s + 4) % 4 == 0 and (s + 4) // 4 in range(2, TILES) else None
+            if even:
+                matmuls(s)
+                if nxt_a is not None:
+                    turn_a(nxt_a)
+                if nxt_b is not None:
+                    turn_b(nxt_b)
+                if s >= 4:
+                    turn_y((s - 4, s - 3))
+            times_chan(s + 1)
+            plus_corr(s)
+            silu(s)
+            times_up(s, nc.gpsimd)
+            round_y(s - 1)
+            store_y(s - 1)
+            if nxt_b is not None:
+                scale_z(nxt_b)
+                group_b(nxt_b)
+            if nxt_a is not None:
+                group_a(nxt_a)
+            if even and s >= 6:
+                quantise_y((s - 6, s - 5))
+            if not even and s >= 5:
+                group_y((s - 5, s - 4))
+            if (s + 5) % 4 == 0 and (s + 5) // 4 in range(2, TILES):
+                quantise_a((s + 5) // 4)
+            if (s + 3) % 4 == 0 and (s + 3) // 4 in range(2, TILES):
+                quantise_b((s + 3) // 4)
+                quantise_z((s + 3) // 4)
+            if even and (s + 2) // 2 < GROUPS:
+                group_u_vector((s + 2) // 2)
+                group_u_scalar((s + 2) // 2)
+            if not even and (s + 1) // 2 < GROUPS:
+                quantise_u((s + 1) // 2)
+            if not even:
+                matmuls(s)
+
+        s = LAST
+        group_y((s - 5, s - 4))
+        turn_y((s - 3, s - 2))
+        plus_corr(s)
+        silu(s)
+        round_y(s - 1)
+        store_y(s - 1)
+        turn_y((s - 1,))
+        group_y((s - 3, s - 2))
+        quantise_y((s - 5, s - 4))
+        times_up(s, nc.vector)
+        store_y(s)
+        dst, src = round_views(s)
+        nc.vector.tensor_copy(out=dst, in_=src)
+        turn_y((s,))
+        group_y((s - 1,))
+        quantise_y((s - 3, s - 2))
+        dst, src = group_y_views((s,))
+        nc.vector.tensor_copy(out=dst, in_=src)
+        quantise_y((s - 1,))
+        quantise_y((s,))

@@ -25,7 +25,8 @@ X_PASSES = K // PASS
 STEPS = [(m, g) for g in range(GROUPS) for m in range(2)] + [(m, g) for m in range(2, TILES) for g in range(GROUPS)]
 LAST = len(STEPS) - 1
 U_SPLIT = 256
-Y_BUFS = 20
+Y_BUFS = 10
+PAIRS = len(STEPS) // 2
 EARLY_SCALE_TILES = 6
 
 
@@ -41,6 +42,12 @@ def tile_frozen_fp4_lowrank_gate_g5_kernel(tc, x, w_words, w_scales, chan, z, la
         bank_a, bank_b, x_grouped_a, x_grouped_b, z_grouped = {}, {}, {}, {}, {}
         base, corr, y, y_sorted, y_bank, y_grouped = {}, {}, {}, {}, {}, {}
 
+        def pair_view(tensor, j):
+            (m, g), (m1, g1) = STEPS[2 * j], STEPS[2 * j + 1]
+            if g1 == g:
+                return tensor[m * P:(m + 2) * P, g * PASS:(g + 1) * PASS].rearrange("(i p) n -> p i n", i=2)
+            return tensor[m * P:(m + 1) * P, g * PASS:(g + 2) * PASS].rearrange("p (i n) -> p i n", i=2)
+
         def load_x(m):
             x_raw[m] = sb.tile([P, K], BF16, name="x_raw", bufs=TILES, align_bytes=64)
             nc.sync.dma_start(out=x_raw[m][:], in_=x[m * P:(m + 1) * P, :])
@@ -49,9 +56,10 @@ def tile_frozen_fp4_lowrank_gate_g5_kernel(tc, x, w_words, w_scales, chan, z, la
             z_raw[m] = sb.tile([P, R], BF16, name="z_raw", bufs=TILES, align_bytes=64)
             nc.sync.dma_start(out=z_raw[m][:], in_=z[m * P:(m + 1) * P, :])
 
-        def load_up(m, half):
-            up_raw[m, half] = sb.tile([P, N // 2], BF16, name="up_raw", bufs=2 * TILES, align_bytes=64)
-            nc.sync.dma_start(out=up_raw[m, half][:], in_=up[m * P:(m + 1) * P, half * (N // 2):(half + 1) * (N // 2)])
+        def load_up(j):
+            (m, g), (m1, g1) = STEPS[2 * j], STEPS[2 * j + 1]
+            up_raw[j] = sb.tile([P, 2, PASS], BF16, name="up_raw", bufs=PAIRS, align_bytes=64)
+            nc.sync.dma_start(out=up_raw[j][:], in_=pair_view(up, j))
 
         def load_u(g):
             u_raw[g] = sb.tile([P, 4, PASS], BF16, name="u_raw", bufs=GROUPS, align_bytes=64)
@@ -72,39 +80,42 @@ def tile_frozen_fp4_lowrank_gate_g5_kernel(tc, x, w_words, w_scales, chan, z, la
         lam_rows = sb.tile([P, 4], BF16, name="lam_rows", align_bytes=64)
         chan_all = sb.tile([P, N], BF16, name="chan_all", align_bytes=64)
 
+        warm = sb.tile([P, 1], F32, name="warm", align_bytes=64)
+        nc.scalar.activation(out=warm[:], in_=ident[:, 0:1], func=SILU)
+
+        nc.sync.dma_start(out=chan_rows[:], in_=chan.rearrange("(p c) -> p c", p=P))
         load_x(0)
         load_u(0)
-        nc.sync.dma_start(out=chan_rows[:], in_=chan.rearrange("(p c) -> p c", p=P))
+        load_z(0)
+        nc.sync.dma_start(out=lam_rows[:], in_=lam.rearrange("(p t) -> p t", t=4))
+        load_x(1)
+        load_z(1)
+        load_w(0)
         for q in range(4):
             nc.sync.dma_start(
                 out=w_plane[32 * q:32 * q + 4, :, :].bitcast(I32),
                 in_=w_scales[:, 4 * q:4 * q + 4, :].rearrange("k r n -> r k n").bitcast(I32),
             )
-        load_z(0)
-        nc.sync.dma_start(out=lam_rows[:], in_=lam.rearrange("(p t) -> p t", t=4))
-        load_w(0)
-        load_x(1)
-        load_z(1)
         load_w(1)
-        load_up(0, 0)
         load_u(1)
-        load_up(1, 0)
+        load_up(0)
         load_w(2)
         load_u(2)
-        load_w(3)
+        load_up(1)
         load_x(2)
-        load_u(3)
         load_z(2)
-        load_up(0, 1)
-        load_up(1, 1)
-        for m in range(2, TILES):
-            if m > 2:
-                load_x(m)
-                load_z(m)
-            load_up(m, 0)
-            load_up(m, 1)
+        load_w(3)
+        load_u(3)
+        load_up(2)
+        for m in range(3, TILES):
+            load_x(m)
+            load_z(m)
+            load_up(2 * m - 3)
+            load_up(2 * m - 2)
+        for j in range(2 * TILES - 3, PAIRS):
+            load_up(j)
 
-        word_stores = [(0, 2, 0, 4), (2, 4, 0, 4), (4, 6, 0, 4), (6, 7, 0, 4), (7, 8, 0, 2), (7, 8, 2, 4)]
+        word_stores = [(0, 2, 0, 4), (2, 4, 0, 4), (4, 5, 0, 4), (5, 6, 0, 4), (6, 7, 0, 4), (7, 8, 0, 4)]
         out_words = {}
         for part in word_stores:
             m0, m1, g0, g1 = part
@@ -151,8 +162,8 @@ def tile_frozen_fp4_lowrank_gate_g5_kernel(tc, x, w_words, w_scales, chan, z, la
             z_grouped[m] = sb.tile([P, PASS], BF16, name="z_grouped", bufs=2, align_bytes=64)
             nc.vector.tensor_tensor(
                 out=z_grouped[m][:].rearrange("p (r h e) -> p r h e", h=2, e=2),
-                in0=bank_b[m][:, 2:4, :].bitcast(BF16).rearrange("p h (r e) -> p r h e", e=2),
-                in1=lam_rows[:].rearrange("p (h e) -> p h e", e=2).unsqueeze(1).to_broadcast([P, P, 2, 2]),
+                in0=lam_rows[:].rearrange("p (h e) -> p h e", e=2).unsqueeze(1).to_broadcast([P, P, 2, 2]),
+                in1=bank_b[m][:, 2:4, :].bitcast(BF16).rearrange("p h (r e) -> p r h e", e=2),
                 op=MULT,
             )
 
@@ -174,9 +185,9 @@ def tile_frozen_fp4_lowrank_gate_g5_kernel(tc, x, w_words, w_scales, chan, z, la
             dst = u_grouped[g][:].rearrange("p (n t) -> p n t", t=4)[:, c0:c1, :]
             return dst.rearrange("p (c i) t -> p c t i", i=4), u_raw[g][:, :, c0:c1].rearrange("p t (c i) -> p c t i", i=4)
 
-        def group_u_vector(g):
+        def group_u_vector(g, split=U_SPLIT):
             u_grouped[g] = sb.tile([P, 4 * PASS], BF16, name="u_grouped", bufs=2, align_bytes=64)
-            dst, src = u_views(g, 0, U_SPLIT)
+            dst, src = u_views(g, 0, split)
             nc.vector.tensor_copy(out=dst, in_=src)
 
         def group_u_scalar(g):
@@ -233,60 +244,51 @@ def tile_frozen_fp4_lowrank_gate_g5_kernel(tc, x, w_words, w_scales, chan, z, la
 
         def times_chan(s):
             g = STEPS[s][1]
-            y[s] = sb.tile([P, PASS], F32, name="y", bufs=Y_BUFS, align_bytes=64)
-            nc.vector.tensor_tensor(out=y[s][:], in0=base[s][:], in1=chan_all[:, g * PASS:(g + 1) * PASS], op=MULT)
+            if s % 2 == 0:
+                y[s // 2] = sb.tile([P, 2, PASS], F32, name="y", bufs=Y_BUFS, align_bytes=64)
+            nc.vector.tensor_tensor(out=y[s // 2][:, s % 2, :], in0=chan_all[:, g * PASS:(g + 1) * PASS], in1=base[s][:], op=MULT)
 
         def plus_corr(s):
-            nc.vector.tensor_tensor(out=y[s][:], in0=corr[s][:], in1=y[s][:], op=ADD)
+            half = y[s // 2][:, s % 2, :]
+            nc.vector.tensor_tensor(out=half, in0=half, in1=corr[s][:], op=ADD)
 
-        def silu(s):
-            nc.scalar.activation(out=y[s][:], in_=y[s][:], func=SILU)
+        def silu(j, i0=0, i1=2):
+            nc.scalar.activation(out=y[j][:, i0:i1, :], in_=y[j][:, i0:i1, :], func=SILU)
 
-        def times_up(s, engine):
-            m, g = STEPS[s]
-            cols = slice((g % 2) * PASS, (g % 2 + 1) * PASS)
-            engine.tensor_tensor(out=y[s][:], in0=y[s][:], in1=up_raw[m, g // 2][:, cols], op=MULT)
+        def times_up(j, engine, i0=0, i1=2):
+            engine.tensor_tensor(out=y[j][:, i0:i1, :], in0=y[j][:, i0:i1, :], in1=up_raw[j][:, i0:i1, :], op=MULT)
 
-        def store_y(s):
-            m, g = STEPS[s]
-            nc.sync.dma_start(out=out_0[m * P:(m + 1) * P, g * PASS:(g + 1) * PASS], in_=y[s][:])
+        def store_y(j, i0=0, i1=2):
+            nc.sync.dma_start(out=pair_view(out_0, j)[:, i0:i1, :], in_=y[j][:, i0:i1, :])
 
-        def round_views(s):
-            y_sorted[s] = sb.tile([P, PASS], BF16, name="y_sorted", bufs=4, align_bytes=64)
-            return (y_sorted[s][:].rearrange("r (h p e) -> r h p e", h=2, e=2),
-                    y[s][:].rearrange("r (p h e) -> r h p e", h=2, e=2))
+        def round_y(j, copy, i0=0, i1=2):
+            if i0 == 0:
+                y_sorted[j] = sb.tile([P, 2, PASS], BF16, name="y_sorted", bufs=3, align_bytes=64)
+            copy(out=y_sorted[j][:, i0:i1, :].rearrange("r i (h p e) -> r i h p e", h=2, e=2),
+                 in_=y[j][:, i0:i1, :].rearrange("r i (p h e) -> r i h p e", h=2, e=2))
 
-        def round_y(s):
-            dst, src = round_views(s)
-            nc.scalar.copy(out=dst, in_=src)
-
-        def turn_y(steps):
-            y_bank[steps] = new_bank()
-            for j, s in enumerate(steps):
-                words = y_sorted[s][:].bitcast(F32)
+        def turn_y(j, i0=0, i1=2):
+            y_bank[j, i0] = new_bank()
+            for i in range(i0, i1):
+                words = y_sorted[j][:, i, :].bitcast(F32)
                 for h in range(2):
-                    nc.tensor.transpose(y_bank[steps][:, 2 * j + h, :], words[:, h * P:(h + 1) * P], ident[:])
+                    nc.tensor.transpose(y_bank[j, i0][:, 2 * i + h, :], words[:, h * P:(h + 1) * P], ident[:])
 
-        def group_y_views(steps):
-            n = len(steps)
-            y_grouped[steps] = sb.tile([P, 2 * PASS], BF16, name="y_grouped", bufs=3, align_bytes=64)
-            return (y_grouped[steps][:, 0:n * PASS].bitcast(F32).rearrange("p (j r h) -> p j r h", j=n, h=2),
-                    y_bank[steps][:, 0:2 * n, :].rearrange("p (j h) r -> p j r h", h=2))
+        def group_y(j, copy, i0=0, i1=2):
+            y_grouped[j, i0] = sb.tile([P, 2, PASS], BF16, name="y_grouped", bufs=4, align_bytes=64)
+            copy(out=y_grouped[j, i0][:, i0:i1, :].bitcast(F32).rearrange("p i (r h) -> p i r h", h=2),
+                 in_=y_bank[j, i0][:, 2 * i0:2 * i1, :].rearrange("p (i h) r -> p i r h", h=2))
 
-        def group_y(steps):
-            dst, src = group_y_views(steps)
-            nc.scalar.copy(out=dst, in_=src)
-
-        def quantise_y(steps):
-            for j, s in enumerate(steps):
-                m, g = STEPS[s]
+        def quantise_y(j, i0=0, i1=2):
+            for i in range(i0, i1):
+                m, g = STEPS[2 * j + i]
                 wpart = [t for t in word_stores if t[0] <= m < t[1] and t[2] <= g < t[3]][0]
                 spart = [t for t in scale_stores if t[0] <= m < t[1]][0]
                 wcol = (m - wpart[0]) * P
                 scol = (m - spart[0]) * P
                 quantise(out_words[wpart][:, g - wpart[2], wcol:wcol + P],
                          out_scales[spart][:, g, scol:scol + P],
-                         y_grouped[steps][:, j * PASS:(j + 1) * PASS])
+                         y_grouped[j, i0][:, i, :])
                 quantised.add((m, g))
                 m0, m1, g0, g1 = wpart
                 if all((a, b) in quantised for a in range(m0, m1) for b in range(g0, g1)):
@@ -303,104 +305,143 @@ def tile_frozen_fp4_lowrank_gate_g5_kernel(tc, x, w_words, w_scales, chan, z, la
                             in_=out_scales[spart][32 * q:32 * q + 4, :, :].bitcast(I32),
                         )
 
-        turn_a(0)
+        on_scalar, on_vector = nc.scalar.copy, nc.vector.tensor_copy
         chan_banks = spread_chan()
+        copy_chan(chan_banks)
+        turn_a(0)
         turn_b(0)
         group_a(0)
-        group_u_vector(0)
-        group_u_scalar(0)
-        quantise_a(0)
-        scale_z(0)
         group_b(0)
-        copy_chan(chan_banks)
-        quantise_u(0)
+        group_u_vector(0, PASS)
+        quantise_a(0)
         quantise_b(0)
+        scale_z(0)
+        quantise_u(0)
         quantise_z(0)
-        base_matmul(0)
-        corr_matmul(0)
         turn_a(1)
         turn_b(1)
-        times_chan(0)
+        base_matmul(0)
+        corr_matmul(0)
         group_a(1)
-        plus_corr(0)
-        quantise_a(1)
         group_b(1)
-        silu(0)
-        times_up(0, nc.gpsimd)
+        quantise_a(1)
         quantise_b(1)
         scale_z(1)
+        times_chan(0)
         base_matmul(1)
-        base_matmul(2)
-        times_chan(1)
         quantise_z(1)
+        plus_corr(0)
         corr_matmul(1)
+        base_matmul(2)
         group_u_vector(1)
         group_u_scalar(1)
+        times_chan(1)
+        base_matmul(3)
+        quantise_u(1)
+        plus_corr(1)
+        corr_matmul(2)
+        corr_matmul(3)
 
-        def matmuls(s):
-            if s + 2 <= LAST:
-                base_matmul(s + 2)
-            if s + 1 <= LAST:
-                corr_matmul(s + 1)
+        for j in range(1, PAIRS - 2):
+            a, b = 2 * j, 2 * j + 1
+            turn_first = [m for m in range(2, TILES) if max(2 * m - 4, 1) == j]
+            turn_second = [m for m in range(2, TILES) if 2 * m - 3 == j]
+            group_first = [m for m in range(2, TILES) if max(2 * m - 4, 1) + 1 == j]
+            group_second = [m for m in range(2, TILES) if 2 * m - 2 == j]
+            quant_first = [m for m in range(2, TILES) if max(2 * m - 4, 1) + 2 == j]
+            quant_second = [m for m in range(2, TILES) if 2 * m - 1 == j]
+            silu(j - 1)
+            times_up(j - 1, nc.gpsimd)
+            times_chan(a)
+            for m in group_second:
+                scale_z(m)
+            if 1 < j < GROUPS:
+                quantise_u(j)
+                corr_matmul(a)
+                corr_matmul(b)
+            for m in quant_first:
+                quantise_a(m)
+            for m in quant_second:
+                quantise_b(m)
+                quantise_z(m)
+            if j >= 5:
+                quantise_y(j - 5)
+            if j + 1 < GROUPS:
+                group_u_vector(j + 1)
+                group_u_scalar(j + 1)
+            for m in group_first:
+                group_a(m)
+            for m in group_second:
+                group_b(m)
+            if j >= 4:
+                group_y(j - 4, on_scalar)
+            base_matmul(a + 2)
+            for m in turn_first:
+                turn_a(m)
+            for m in turn_second:
+                turn_b(m)
+            if j >= 3:
+                turn_y(j - 3)
+            if j >= 2:
+                round_y(j - 2, on_scalar)
+            times_chan(b)
+            plus_corr(a)
+            plus_corr(b)
+            store_y(j - 1)
+            base_matmul(b + 2)
+            if j == PAIRS - 3:
+                turn_y(j - 2)
+            if j + 1 >= GROUPS:
+                corr_matmul(a + 2)
+                corr_matmul(b + 2)
 
-        for s in range(1, LAST):
-            even = s % 2 == 0
-            nxt_a = (s + 6) // 4 if (s + 6) % 4 == 0 and (s + 6) // 4 in range(2, TILES) else None
-            nxt_b = (s + 4) // 4 if (s + 4) % 4 == 0 and (s + 4) // 4 in range(2, TILES) else None
-            if even:
-                matmuls(s)
-                if nxt_a is not None:
-                    turn_a(nxt_a)
-                if nxt_b is not None:
-                    turn_b(nxt_b)
-                if s >= 4:
-                    turn_y((s - 4, s - 3))
-            times_chan(s + 1)
-            plus_corr(s)
-            silu(s)
-            times_up(s, nc.gpsimd)
-            round_y(s - 1)
-            store_y(s - 1)
-            if nxt_b is not None:
-                scale_z(nxt_b)
-                group_b(nxt_b)
-            if nxt_a is not None:
-                group_a(nxt_a)
-            if even and s >= 6:
-                quantise_y((s - 6, s - 5))
-            if not even and s >= 5:
-                group_y((s - 5, s - 4))
-            if (s + 5) % 4 == 0 and (s + 5) // 4 in range(2, TILES):
-                quantise_a((s + 5) // 4)
-            if (s + 3) % 4 == 0 and (s + 3) // 4 in range(2, TILES):
-                quantise_b((s + 3) // 4)
-                quantise_z((s + 3) // 4)
-            if even and (s + 2) // 2 < GROUPS:
-                group_u_vector((s + 2) // 2)
-                group_u_scalar((s + 2) // 2)
-            if not even and (s + 1) // 2 < GROUPS:
-                quantise_u((s + 1) // 2)
-            if not even:
-                matmuls(s)
-
-        s = LAST
-        group_y((s - 5, s - 4))
-        turn_y((s - 3, s - 2))
-        plus_corr(s)
-        silu(s)
-        round_y(s - 1)
-        store_y(s - 1)
-        turn_y((s - 1,))
-        group_y((s - 3, s - 2))
-        quantise_y((s - 5, s - 4))
-        times_up(s, nc.vector)
-        store_y(s)
-        dst, src = round_views(s)
-        nc.vector.tensor_copy(out=dst, in_=src)
-        turn_y((s,))
-        group_y((s - 1,))
-        quantise_y((s - 3, s - 2))
-        dst, src = group_y_views((s,))
-        nc.vector.tensor_copy(out=dst, in_=src)
-        quantise_y((s - 1,))
-        quantise_y((s,))
+        silu(13)
+        times_up(13, nc.gpsimd)
+        times_chan(28)
+        quantise_y(9)
+        base_matmul(30)
+        round_y(12, on_scalar)
+        group_y(10, on_scalar)
+        group_y(11, on_scalar)
+        times_chan(29)
+        plus_corr(28)
+        plus_corr(29)
+        store_y(13)
+        base_matmul(31)
+        turn_y(12)
+        corr_matmul(30)
+        corr_matmul(31)
+        silu(14)
+        times_up(14, nc.gpsimd, 0, 1)
+        times_chan(30)
+        quantise_y(10)
+        times_chan(31)
+        times_up(14, nc.vector, 1, 2)
+        quantise_y(11)
+        store_y(14)
+        round_y(13, on_scalar)
+        turn_y(13)
+        group_y(12, on_scalar)
+        plus_corr(30)
+        plus_corr(31)
+        silu(15, 0, 1)
+        silu(15, 1, 2)
+        quantise_y(12)
+        times_up(15, nc.vector, 0, 1)
+        store_y(15, 0, 1)
+        times_up(15, nc.vector, 1, 2)
+        store_y(15, 1, 2)
+        round_y(14, on_scalar)
+        turn_y(14)
+        group_y(13, on_scalar)
+        round_y(15, on_vector, 0, 1)
+        turn_y(15, 0, 1)
+        round_y(15, on_vector, 1, 2)
+        turn_y(15, 1, 2)
+        group_y(14, on_scalar)
+        quantise_y(13)
+        group_y(15, on_vector, 0, 1)
+        group_y(15, on_scalar, 1, 2)
+        quantise_y(14)
+        quantise_y(15, 0, 1)
+        quantise_y(15, 1, 2)

@@ -74,8 +74,24 @@ def tile_frozen_fp4_lowrank_gate_g5_kernel(tc, x, w_words, w_scales, chan, z, la
 
         ident = sb.tile([P, P], F32, name="ident", align_bytes=64)
         make_identity(nc, ident[:])
-        w_plane = sb.tile([P, X_PASSES, N], U8, name="w_plane", align_bytes=64)
-        nc.vector.memset(w_plane[:].bitcast(I32), 0)
+        w_plane = {}
+        for half in range(2):
+            w_plane[half] = sb.tile([P, X_PASSES, N // 2], U8, name="w_plane", bufs=2, align_bytes=64)
+            nc.vector.memset(w_plane[half][:].bitcast(I32), 0)
+
+        def load_w_scales(half):
+            for q in range(4):
+                nc.sync.dma_start(
+                    out=w_plane[half][32 * q:32 * q + 4, :, :].bitcast(I32),
+                    in_=w_scales[:, 4 * q:4 * q + 4, half * (N // 2):(half + 1) * (N // 2)].rearrange("k r n -> r k n").bitcast(I32),
+                )
+
+        def load_chan():
+            nc.sync.dma_start(out=chan_rows[:], in_=chan.rearrange("(p c) -> p c", p=P))
+
+        def load_lam():
+            nc.sync.dma_start(out=lam_rows[:], in_=lam.rearrange("(p t) -> p t", t=4))
+
         chan_rows = sb.tile([P, N // P], BF16, name="chan_rows", align_bytes=64)
         lam_rows = sb.tile([P, 4], BF16, name="lam_rows", align_bytes=64)
         chan_all = sb.tile([P, N], BF16, name="chan_all", align_bytes=64)
@@ -83,29 +99,26 @@ def tile_frozen_fp4_lowrank_gate_g5_kernel(tc, x, w_words, w_scales, chan, z, la
         warm = sb.tile([P, 1], F32, name="warm", align_bytes=64)
         nc.scalar.activation(out=warm[:], in_=ident[:, 0:1], func=SILU)
 
-        nc.sync.dma_start(out=chan_rows[:], in_=chan.rearrange("(p c) -> p c", p=P))
+        load_chan()
         load_x(0)
         load_u(0)
         load_z(0)
-        nc.sync.dma_start(out=lam_rows[:], in_=lam.rearrange("(p t) -> p t", t=4))
+        load_lam()
         load_x(1)
         load_z(1)
         load_w(0)
-        for q in range(4):
-            nc.sync.dma_start(
-                out=w_plane[32 * q:32 * q + 4, :, :].bitcast(I32),
-                in_=w_scales[:, 4 * q:4 * q + 4, :].rearrange("k r n -> r k n").bitcast(I32),
-            )
-        load_w(1)
+        load_w_scales(0)
         load_u(1)
+        load_w(1)
         load_up(0)
-        load_w(2)
         load_u(2)
-        load_up(1)
+        load_w_scales(1)
+        load_w(2)
         load_x(2)
         load_z(2)
-        load_w(3)
         load_u(3)
+        load_up(1)
+        load_w(3)
         load_up(2)
         for m in range(3, TILES):
             load_x(m)
@@ -115,12 +128,12 @@ def tile_frozen_fp4_lowrank_gate_g5_kernel(tc, x, w_words, w_scales, chan, z, la
         for j in range(2 * TILES - 3, PAIRS):
             load_up(j)
 
-        word_stores = [(0, 2, 0, 4), (2, 4, 0, 4), (4, 5, 0, 4), (5, 6, 0, 4), (6, 7, 0, 4), (7, 8, 0, 4)]
+        word_stores = [(0, 2, 0, 4), (2, 4, 0, 4), (4, 5, 0, 4), (5, 6, 0, 4), (6, 7, 0, 4), (7, 8, 0, 2), (7, 8, 2, 4)]
         out_words = {}
         for part in word_stores:
             m0, m1, g0, g1 = part
             out_words[part] = sb.tile([P, g1 - g0, (m1 - m0) * P], U32, name="out_words_%d_%d" % (m0, g0), align_bytes=64)
-        scale_stores = [(0, EARLY_SCALE_TILES), (EARLY_SCALE_TILES, TILES)]
+        scale_stores = [(0, 4), (4, 6), (6, 8)]
         out_scales = {}
         for part in scale_stores:
             out_scales[part] = sb.tile([P, GROUPS, (part[1] - part[0]) * P], U8, name="out_scales_%d" % part[0], align_bytes=64)
@@ -185,14 +198,14 @@ def tile_frozen_fp4_lowrank_gate_g5_kernel(tc, x, w_words, w_scales, chan, z, la
             dst = u_grouped[g][:].rearrange("p (n t) -> p n t", t=4)[:, c0:c1, :]
             return dst.rearrange("p (c i) t -> p c t i", i=4), u_raw[g][:, :, c0:c1].rearrange("p t (c i) -> p c t i", i=4)
 
-        def group_u_vector(g, split=U_SPLIT):
+        def group_u(g, split):
             u_grouped[g] = sb.tile([P, 4 * PASS], BF16, name="u_grouped", bufs=2, align_bytes=64)
-            dst, src = u_views(g, 0, split)
-            nc.vector.tensor_copy(out=dst, in_=src)
-
-        def group_u_scalar(g):
-            dst, src = u_views(g, U_SPLIT, PASS)
-            nc.scalar.copy(out=dst, in_=src)
+            if split > 0:
+                dst, src = u_views(g, 0, split)
+                nc.vector.tensor_copy(out=dst, in_=src)
+            if split < PASS:
+                dst, src = u_views(g, split, PASS)
+                nc.scalar.copy(out=dst, in_=src)
 
         def quantise_u(g):
             u_codes[g] = sb.tile([P, PASS], U32, name="u_codes", bufs=GROUPS, align_bytes=64)
@@ -224,7 +237,7 @@ def tile_frozen_fp4_lowrank_gate_g5_kernel(tc, x, w_words, w_scales, chan, z, la
                     lhsT=act_codes[m][:, k * P:(k + 1) * P].bitcast(FP8X4),
                     lhsT_scale=act_scales[m][:, k * P:(k + 1) * P],
                     rhs=w_codes[g][:, k, :].bitcast(FP4X4),
-                    rhs_scale=w_plane[:, k, g * PASS:(g + 1) * PASS],
+                    rhs_scale=w_plane[g // 2][:, k, (g % 2) * PASS:(g % 2 + 1) * PASS],
                     start=(k == 0),
                     stop=(k == X_PASSES - 1),
                 )
@@ -312,7 +325,7 @@ def tile_frozen_fp4_lowrank_gate_g5_kernel(tc, x, w_words, w_scales, chan, z, la
         turn_b(0)
         group_a(0)
         group_b(0)
-        group_u_vector(0, PASS)
+        group_u(0, PASS)
         quantise_a(0)
         quantise_b(0)
         scale_z(0)
@@ -324,23 +337,19 @@ def tile_frozen_fp4_lowrank_gate_g5_kernel(tc, x, w_words, w_scales, chan, z, la
         corr_matmul(0)
         group_a(1)
         group_b(1)
+        group_u(1, 0)
         quantise_a(1)
         quantise_b(1)
+        base_matmul(1)
         scale_z(1)
         times_chan(0)
-        base_matmul(1)
         quantise_z(1)
-        plus_corr(0)
         corr_matmul(1)
         base_matmul(2)
-        group_u_vector(1)
-        group_u_scalar(1)
         times_chan(1)
+        plus_corr(0)
         base_matmul(3)
-        quantise_u(1)
         plus_corr(1)
-        corr_matmul(2)
-        corr_matmul(3)
 
         for j in range(1, PAIRS - 2):
             a, b = 2 * j, 2 * j + 1
@@ -350,12 +359,12 @@ def tile_frozen_fp4_lowrank_gate_g5_kernel(tc, x, w_words, w_scales, chan, z, la
             group_second = [m for m in range(2, TILES) if 2 * m - 2 == j]
             quant_first = [m for m in range(2, TILES) if max(2 * m - 4, 1) + 2 == j]
             quant_second = [m for m in range(2, TILES) if 2 * m - 1 == j]
+            if j == GROUPS - 1:
+                group_a(j)
             silu(j - 1)
             times_up(j - 1, nc.gpsimd)
             times_chan(a)
-            for m in group_second:
-                scale_z(m)
-            if 1 < j < GROUPS:
+            if j < GROUPS:
                 quantise_u(j)
                 corr_matmul(a)
                 corr_matmul(b)
@@ -367,10 +376,10 @@ def tile_frozen_fp4_lowrank_gate_g5_kernel(tc, x, w_words, w_scales, chan, z, la
             if j >= 5:
                 quantise_y(j - 5)
             if j + 1 < GROUPS:
-                group_u_vector(j + 1)
-                group_u_scalar(j + 1)
+                group_u(j + 1, (0, 320)[j - 1])
             for m in group_first:
-                group_a(m)
+                if j != GROUPS - 1:
+                    group_a(m)
             for m in group_second:
                 group_b(m)
             if j >= 4:
@@ -385,6 +394,8 @@ def tile_frozen_fp4_lowrank_gate_g5_kernel(tc, x, w_words, w_scales, chan, z, la
             if j >= 2:
                 round_y(j - 2, on_scalar)
             times_chan(b)
+            for m in group_second:
+                scale_z(m)
             plus_corr(a)
             plus_corr(b)
             store_y(j - 1)
@@ -411,13 +422,14 @@ def tile_frozen_fp4_lowrank_gate_g5_kernel(tc, x, w_words, w_scales, chan, z, la
         turn_y(12)
         corr_matmul(30)
         corr_matmul(31)
-        silu(14)
-        times_up(14, nc.gpsimd, 0, 1)
+        silu(14, 1, 2)
+        silu(14, 0, 1)
         times_chan(30)
         quantise_y(10)
-        times_chan(31)
-        times_up(14, nc.vector, 1, 2)
         quantise_y(11)
+        times_up(14, nc.vector, 1, 2)
+        times_up(14, nc.gpsimd, 0, 1)
+        times_chan(31)
         store_y(14)
         round_y(13, on_scalar)
         turn_y(13)

@@ -19,34 +19,60 @@ SILU = mybir.ActivationFunctionType.Silu
 
 P = 128
 PASS = 512
+QUADRANTS = 4
 TILES = M // P
 GROUPS = N // PASS
 X_PASSES = K // PASS
-STEPS = [(m, g) for g in range(GROUPS) for m in range(2)] + [(m, g) for m in range(2, TILES) for g in range(GROUPS)]
-LAST = len(STEPS) - 1
-U_SPLIT = 256
-Y_BUFS = 10
+
+HEAD_TILES = 2
+STEPS = [(m, g) for g in range(GROUPS) for m in range(HEAD_TILES)]
+STEPS = STEPS + [(m, g) for m in range(HEAD_TILES, TILES) for g in range(GROUPS)]
 PAIRS = len(STEPS) // 2
-EARLY_SCALE_TILES = 6
+SPLIT_PAIR = PAIRS - 2
+
+Y_BUFS = 10
+U2_EARLY = 192
+U3_VECTOR = 320
+
+WORD_PARTS = [(0, 2, 0, 4), (2, 4, 0, 4), (4, 5, 0, 4), (5, 6, 0, 4), (6, 7, 0, 4), (7, 8, 0, 2), (7, 8, 2, 4)]
+SCALE_PARTS = [(0, 4), (4, 6), (6, 8)]
 
 
 def tile_frozen_fp4_lowrank_gate_g5_kernel(tc, x, w_words, w_scales, chan, z, lam, u, up, out_0, out_1, out_2):
     nc = tc.nc
+    on_scalar, on_vector = nc.scalar.copy, nc.vector.tensor_copy
     with ExitStack() as ctx:
         sb = ctx.enter_context(tc.tile_pool(name="sb", bufs=1))
         ps = ctx.enter_context(tc.psum_pool(name="ps", bufs=2))
         ctx.enter_context(tc.manual_schedule())
 
-        x_raw, z_raw, up_raw, u_raw, w_codes = {}, {}, {}, {}, {}
-        act_codes, act_scales, u_codes, u_scales, u_grouped = {}, {}, {}, {}, {}
-        bank_a, bank_b, x_grouped_a, x_grouped_b, z_grouped = {}, {}, {}, {}, {}
+        x_raw, z_raw, up_raw, u_raw, w_codes, w_plane = {}, {}, {}, {}, {}, {}
+        bank_a, bank_b, x_grouped_a, x_grouped_b, z_grouped, u_grouped = {}, {}, {}, {}, {}, {}
+        act_codes, act_scales, u_codes, u_scales = {}, {}, {}, {}
         base, corr, y, y_sorted, y_bank, y_grouped = {}, {}, {}, {}, {}, {}
+        out_words, out_scales, quantised = {}, {}, set()
 
         def pair_view(tensor, j):
-            (m, g), (m1, g1) = STEPS[2 * j], STEPS[2 * j + 1]
-            if g1 == g:
-                return tensor[m * P:(m + 2) * P, g * PASS:(g + 1) * PASS].rearrange("(i p) n -> p i n", i=2)
-            return tensor[m * P:(m + 1) * P, g * PASS:(g + 2) * PASS].rearrange("p (i n) -> p i n", i=2)
+            (m, g), (m_next, g_next) = STEPS[2 * j], STEPS[2 * j + 1]
+            if g_next == g:
+                return tensor[m * P:(m_next + 1) * P, g * PASS:(g + 1) * PASS].rearrange("(i p) n -> p i n", i=2)
+            return tensor[m * P:(m + 1) * P, g * PASS:(g_next + 1) * PASS].rearrange("p (i n) -> p i n", i=2)
+
+        def step_rows(tiles, name, dtype, bufs, j, i0, i1):
+            split = j >= SPLIT_PAIR
+            key = (j, i0 if split else 0)
+            if key not in tiles:
+                if split:
+                    tiles[key] = sb.tile([P, 1, PASS], dtype, name=name + "_step", bufs=4, align_bytes=64)
+                else:
+                    tiles[key] = sb.tile([P, 2, PASS], dtype, name=name, bufs=bufs, align_bytes=64)
+            return tiles[key][:, i0 - key[1]:i1 - key[1], :]
+
+        def y_rows(j, i0, i1):
+            return step_rows(y, "y", F32, Y_BUFS, j, i0, i1)
+
+        def y_sorted_rows(j, i0, i1):
+            return step_rows(y_sorted, "y_sorted", BF16, 3, j, i0, i1)
 
         def load_x(m):
             x_raw[m] = sb.tile([P, K], BF16, name="x_raw", bufs=TILES, align_bytes=64)
@@ -57,7 +83,6 @@ def tile_frozen_fp4_lowrank_gate_g5_kernel(tc, x, w_words, w_scales, chan, z, la
             nc.sync.dma_start(out=z_raw[m][:], in_=z[m * P:(m + 1) * P, :])
 
         def load_up(j):
-            (m, g), (m1, g1) = STEPS[2 * j], STEPS[2 * j + 1]
             up_raw[j] = sb.tile([P, 2, PASS], BF16, name="up_raw", bufs=PAIRS, align_bytes=64)
             nc.sync.dma_start(out=up_raw[j][:], in_=pair_view(up, j))
 
@@ -72,26 +97,19 @@ def tile_frozen_fp4_lowrank_gate_g5_kernel(tc, x, w_words, w_scales, chan, z, la
                 in_=w_words.rearrange("k p b -> p k b")[:, :, g * 2 * PASS:(g + 1) * 2 * PASS].bitcast(I32),
             )
 
+        def load_w_scales(half):
+            cols = slice(half * (N // 2), (half + 1) * (N // 2))
+            for q in range(QUADRANTS):
+                nc.sync.dma_start(
+                    out=w_plane[half][32 * q:32 * q + 4, :, :].bitcast(I32),
+                    in_=w_scales[:, 4 * q:4 * q + 4, cols].rearrange("k r n -> r k n").bitcast(I32),
+                )
+
         ident = sb.tile([P, P], F32, name="ident", align_bytes=64)
         make_identity(nc, ident[:])
-        w_plane = {}
         for half in range(2):
             w_plane[half] = sb.tile([P, X_PASSES, N // 2], U8, name="w_plane", bufs=2, align_bytes=64)
             nc.vector.memset(w_plane[half][:].bitcast(I32), 0)
-
-        def load_w_scales(half):
-            for q in range(4):
-                nc.sync.dma_start(
-                    out=w_plane[half][32 * q:32 * q + 4, :, :].bitcast(I32),
-                    in_=w_scales[:, 4 * q:4 * q + 4, half * (N // 2):(half + 1) * (N // 2)].rearrange("k r n -> r k n").bitcast(I32),
-                )
-
-        def load_chan():
-            nc.sync.dma_start(out=chan_rows[:], in_=chan.rearrange("(p c) -> p c", p=P))
-
-        def load_lam():
-            nc.sync.dma_start(out=lam_rows[:], in_=lam.rearrange("(p t) -> p t", t=4))
-
         chan_rows = sb.tile([P, N // P], BF16, name="chan_rows", align_bytes=64)
         lam_rows = sb.tile([P, 4], BF16, name="lam_rows", align_bytes=64)
         chan_all = sb.tile([P, N], BF16, name="chan_all", align_bytes=64)
@@ -99,19 +117,19 @@ def tile_frozen_fp4_lowrank_gate_g5_kernel(tc, x, w_words, w_scales, chan, z, la
         warm = sb.tile([P, 1], F32, name="warm", align_bytes=64)
         nc.scalar.activation(out=warm[:], in_=ident[:, 0:1], func=SILU)
 
-        load_chan()
+        nc.sync.dma_start(out=chan_rows[:], in_=chan.rearrange("(p c) -> p c", p=P))
         load_x(0)
         load_u(0)
         load_z(0)
-        load_lam()
+        nc.sync.dma_start(out=lam_rows[:], in_=lam.rearrange("(p t) -> p t", t=4))
         load_x(1)
         load_z(1)
         load_w(0)
         load_w_scales(0)
         load_u(1)
         load_w(1)
-        load_up(0)
         load_u(2)
+        load_up(0)
         load_w_scales(1)
         load_w(2)
         load_x(2)
@@ -119,64 +137,61 @@ def tile_frozen_fp4_lowrank_gate_g5_kernel(tc, x, w_words, w_scales, chan, z, la
         load_u(3)
         load_up(1)
         load_w(3)
-        load_up(2)
         for m in range(3, TILES):
             load_x(m)
             load_z(m)
+            load_up(2 * m - 4)
             load_up(2 * m - 3)
-            load_up(2 * m - 2)
-        for j in range(2 * TILES - 3, PAIRS):
+        for j in range(2 * TILES - 4, PAIRS):
             load_up(j)
 
-        word_stores = [(0, 2, 0, 4), (2, 4, 0, 4), (4, 5, 0, 4), (5, 6, 0, 4), (6, 7, 0, 4), (7, 8, 0, 2), (7, 8, 2, 4)]
-        out_words = {}
-        for part in word_stores:
+        for part in WORD_PARTS:
             m0, m1, g0, g1 = part
             out_words[part] = sb.tile([P, g1 - g0, (m1 - m0) * P], U32, name="out_words_%d_%d" % (m0, g0), align_bytes=64)
-        scale_stores = [(0, 4), (4, 6), (6, 8)]
-        out_scales = {}
-        for part in scale_stores:
-            out_scales[part] = sb.tile([P, GROUPS, (part[1] - part[0]) * P], U8, name="out_scales_%d" % part[0], align_bytes=64)
-        quantised = set()
+        for part in SCALE_PARTS:
+            m0, m1 = part
+            out_scales[part] = sb.tile([P, GROUPS, (m1 - m0) * P], U8, name="out_scales_%d" % m0, align_bytes=64)
 
         def new_bank():
             return ps.tile([P, 4, P], F32, name="turn_bank", bufs=4)
 
-        def turn_words(bank, slot, words):
+        def turn_pass(bank, quarter, words):
             for h in range(2):
-                nc.tensor.transpose(bank[:, slot + h, :], words[:, h:2 * P:2], ident[:])
+                nc.tensor.transpose(bank[:, quarter + h, :], words[:, h:2 * P:2], ident[:])
 
         def turn_a(m):
             bank_a[m] = new_bank()
             words = x_raw[m][:].bitcast(F32)
-            turn_words(bank_a[m], 0, words[:, 0:2 * P])
-            turn_words(bank_a[m], 2, words[:, 2 * P:4 * P])
+            turn_pass(bank_a[m], 0, words[:, 0:2 * P])
+            turn_pass(bank_a[m], 2, words[:, 2 * P:4 * P])
 
         def turn_b(m):
             bank_b[m] = new_bank()
-            turn_words(bank_b[m], 0, x_raw[m][:].bitcast(F32)[:, 4 * P:6 * P])
-            turn_words(bank_b[m], 2, z_raw[m][:].bitcast(F32))
+            turn_pass(bank_b[m], 0, x_raw[m][:].bitcast(F32)[:, 4 * P:6 * P])
+            turn_pass(bank_b[m], 2, z_raw[m][:].bitcast(F32))
 
-        def group_a(m):
-            x_grouped_a[m] = sb.tile([P, 2 * PASS], BF16, name="x_grouped_a", bufs=2, align_bytes=64)
-            nc.scalar.copy(
-                out=x_grouped_a[m][:].bitcast(F32).rearrange("p (k r h) -> p k r h", k=2, h=2),
-                in_=bank_a[m][:].rearrange("p (k h) r -> p k r h", h=2),
+        def group_a(m, k0=0, k1=2):
+            if k0 == 0:
+                x_grouped_a[m] = sb.tile([P, 2 * PASS], BF16, name="x_grouped_a", bufs=2, align_bytes=64)
+            on_scalar(
+                out=x_grouped_a[m][:].bitcast(F32).rearrange("p (k r h) -> p k r h", k=2, h=2)[:, k0:k1],
+                in_=bank_a[m][:].rearrange("p (k h) r -> p k r h", h=2)[:, k0:k1],
             )
 
         def group_b(m):
             x_grouped_b[m] = sb.tile([P, PASS], BF16, name="x_grouped_b", bufs=2, align_bytes=64)
-            nc.scalar.copy(
+            on_scalar(
                 out=x_grouped_b[m][:].bitcast(F32).rearrange("p (r h) -> p r h", h=2),
                 in_=bank_b[m][:, 0:2, :].rearrange("p h r -> p r h"),
             )
 
-        def scale_z(m):
-            z_grouped[m] = sb.tile([P, PASS], BF16, name="z_grouped", bufs=2, align_bytes=64)
+        def scale_z(m, r0=0, r1=P):
+            if r0 == 0:
+                z_grouped[m] = sb.tile([P, PASS], BF16, name="z_grouped", bufs=2, align_bytes=64)
             nc.vector.tensor_tensor(
-                out=z_grouped[m][:].rearrange("p (r h e) -> p r h e", h=2, e=2),
-                in0=lam_rows[:].rearrange("p (h e) -> p h e", e=2).unsqueeze(1).to_broadcast([P, P, 2, 2]),
-                in1=bank_b[m][:, 2:4, :].bitcast(BF16).rearrange("p h (r e) -> p r h e", e=2),
+                out=z_grouped[m][:].rearrange("p (r h e) -> p r h e", h=2, e=2)[:, r0:r1],
+                in0=lam_rows[:].rearrange("p (h e) -> p h e", e=2).unsqueeze(1).to_broadcast([P, r1 - r0, 2, 2]),
+                in1=bank_b[m][:, 2:4, :].bitcast(BF16).rearrange("p h (r e) -> p r h e", e=2)[:, r0:r1],
                 op=MULT,
             )
 
@@ -194,18 +209,12 @@ def tile_frozen_fp4_lowrank_gate_g5_kernel(tc, x, w_words, w_scales, chan, z, la
         def quantise_z(m):
             quantise(act_codes[m][:, 3 * P:4 * P], act_scales[m][:, 3 * P:4 * P], z_grouped[m][:])
 
-        def u_views(g, c0, c1):
-            dst = u_grouped[g][:].rearrange("p (n t) -> p n t", t=4)[:, c0:c1, :]
-            return dst.rearrange("p (c i) t -> p c t i", i=4), u_raw[g][:, :, c0:c1].rearrange("p t (c i) -> p c t i", i=4)
-
-        def group_u(g, split):
-            u_grouped[g] = sb.tile([P, 4 * PASS], BF16, name="u_grouped", bufs=2, align_bytes=64)
-            if split > 0:
-                dst, src = u_views(g, 0, split)
-                nc.vector.tensor_copy(out=dst, in_=src)
-            if split < PASS:
-                dst, src = u_views(g, split, PASS)
-                nc.scalar.copy(out=dst, in_=src)
+        def group_u(g, copy, c0, c1):
+            if c0 == 0:
+                u_grouped[g] = sb.tile([P, 4 * PASS], BF16, name="u_grouped", bufs=3, align_bytes=64)
+            columns = u_grouped[g][:].rearrange("p (n t) -> p n t", t=4)[:, c0:c1, :]
+            copy(out=columns.rearrange("p (c i) t -> p c t i", i=4),
+                 in_=u_raw[g][:, :, c0:c1].rearrange("p t (c i) -> p c t i", i=4))
 
         def quantise_u(g):
             u_codes[g] = sb.tile([P, PASS], U32, name="u_codes", bufs=GROUPS, align_bytes=64)
@@ -214,19 +223,12 @@ def tile_frozen_fp4_lowrank_gate_g5_kernel(tc, x, w_words, w_scales, chan, z, la
 
         def spread_chan():
             words = chan_rows[:].bitcast(F32)
-            banks = []
-            for b in range(2):
-                bank = new_bank()
-                for j in range(4):
-                    c = 4 * b + j
-                    nc.tensor.transpose(bank[:, j, :], words[:, c:c + 1].to_broadcast([P, P]), ident[:])
-                banks.append(bank)
-            return banks
-
-        def copy_chan(banks):
-            dst = chan_all[:].bitcast(F32).rearrange("q (p c) -> q p c", p=P)
-            for b in range(2):
-                nc.scalar.copy(out=dst[:, :, 4 * b:4 * b + 4], in_=banks[b][:].rearrange("q j p -> q p j"))
+            spread = chan_all[:].bitcast(F32).rearrange("q (p c) -> q p c", p=P)
+            banks = [new_bank(), new_bank()]
+            for c in range(8):
+                nc.tensor.transpose(banks[c // 4][:, c % 4, :], words[:, c:c + 1].to_broadcast([P, P]), ident[:])
+            for i in range(2):
+                on_scalar(out=spread[:, :, 4 * i:4 * i + 4], in_=banks[i][:].rearrange("q c p -> q p c"))
 
         def base_matmul(s):
             m, g = STEPS[s]
@@ -257,75 +259,78 @@ def tile_frozen_fp4_lowrank_gate_g5_kernel(tc, x, w_words, w_scales, chan, z, la
 
         def times_chan(s):
             g = STEPS[s][1]
-            if s % 2 == 0:
-                y[s // 2] = sb.tile([P, 2, PASS], F32, name="y", bufs=Y_BUFS, align_bytes=64)
-            nc.vector.tensor_tensor(out=y[s // 2][:, s % 2, :], in0=chan_all[:, g * PASS:(g + 1) * PASS], in1=base[s][:], op=MULT)
+            rows = y_rows(s // 2, s % 2, s % 2 + 1)[:, 0, :]
+            nc.vector.tensor_tensor(out=rows, in0=chan_all[:, g * PASS:(g + 1) * PASS], in1=base[s][:], op=MULT)
 
         def plus_corr(s):
-            half = y[s // 2][:, s % 2, :]
-            nc.vector.tensor_tensor(out=half, in0=half, in1=corr[s][:], op=ADD)
+            rows = y_rows(s // 2, s % 2, s % 2 + 1)[:, 0, :]
+            nc.vector.tensor_tensor(out=rows, in0=rows, in1=corr[s][:], op=ADD)
 
         def silu(j, i0=0, i1=2):
-            nc.scalar.activation(out=y[j][:, i0:i1, :], in_=y[j][:, i0:i1, :], func=SILU)
+            nc.scalar.activation(out=y_rows(j, i0, i1), in_=y_rows(j, i0, i1), func=SILU)
 
         def times_up(j, engine, i0=0, i1=2):
-            engine.tensor_tensor(out=y[j][:, i0:i1, :], in0=y[j][:, i0:i1, :], in1=up_raw[j][:, i0:i1, :], op=MULT)
+            engine.tensor_tensor(out=y_rows(j, i0, i1), in0=y_rows(j, i0, i1), in1=up_raw[j][:, i0:i1, :], op=MULT)
 
         def store_y(j, i0=0, i1=2):
-            nc.sync.dma_start(out=pair_view(out_0, j)[:, i0:i1, :], in_=y[j][:, i0:i1, :])
+            nc.sync.dma_start(out=pair_view(out_0, j)[:, i0:i1, :], in_=y_rows(j, i0, i1))
 
         def round_y(j, copy, i0=0, i1=2):
-            if i0 == 0:
-                y_sorted[j] = sb.tile([P, 2, PASS], BF16, name="y_sorted", bufs=3, align_bytes=64)
-            copy(out=y_sorted[j][:, i0:i1, :].rearrange("r i (h p e) -> r i h p e", h=2, e=2),
-                 in_=y[j][:, i0:i1, :].rearrange("r i (p h e) -> r i h p e", h=2, e=2))
+            copy(out=y_sorted_rows(j, i0, i1).rearrange("r i (h p e) -> r i h p e", h=2, e=2),
+                 in_=y_rows(j, i0, i1).rearrange("r i (p h e) -> r i h p e", h=2, e=2))
 
         def turn_y(j, i0=0, i1=2):
-            y_bank[j, i0] = new_bank()
+            bank = new_bank()
             for i in range(i0, i1):
-                words = y_sorted[j][:, i, :].bitcast(F32)
+                y_bank[j, i] = bank
+                words = y_sorted_rows(j, i, i + 1)[:, 0, :].bitcast(F32)
                 for h in range(2):
-                    nc.tensor.transpose(y_bank[j, i0][:, 2 * i + h, :], words[:, h * P:(h + 1) * P], ident[:])
+                    nc.tensor.transpose(bank[:, 2 * i + h, :], words[:, h * P:(h + 1) * P], ident[:])
 
         def group_y(j, copy, i0=0, i1=2):
-            y_grouped[j, i0] = sb.tile([P, 2, PASS], BF16, name="y_grouped", bufs=4, align_bytes=64)
-            copy(out=y_grouped[j, i0][:, i0:i1, :].bitcast(F32).rearrange("p i (r h) -> p i r h", h=2),
+            if i0 == 0:
+                y_grouped[j] = sb.tile([P, 2, PASS], BF16, name="y_grouped", bufs=4, align_bytes=64)
+            copy(out=y_grouped[j][:, i0:i1, :].bitcast(F32).rearrange("p i (r h) -> p i r h", h=2),
                  in_=y_bank[j, i0][:, 2 * i0:2 * i1, :].rearrange("p (i h) r -> p i r h", h=2))
 
-        def quantise_y(j, i0=0, i1=2):
-            for i in range(i0, i1):
-                m, g = STEPS[2 * j + i]
-                wpart = [t for t in word_stores if t[0] <= m < t[1] and t[2] <= g < t[3]][0]
-                spart = [t for t in scale_stores if t[0] <= m < t[1]][0]
-                wcol = (m - wpart[0]) * P
-                scol = (m - spart[0]) * P
-                quantise(out_words[wpart][:, g - wpart[2], wcol:wcol + P],
-                         out_scales[spart][:, g, scol:scol + P],
-                         y_grouped[j, i0][:, i, :])
-                quantised.add((m, g))
-                m0, m1, g0, g1 = wpart
-                if all((a, b) in quantised for a in range(m0, m1) for b in range(g0, g1)):
-                    nc.sync.dma_start(
-                        out=out_1[g0:g1].rearrange("g p m t -> p g (m t)")[:, :, m0 * P * 4:m1 * P * 4].bitcast(I32),
-                        in_=out_words[wpart][:].bitcast(I32),
-                    )
-                m0, m1 = spart
-                if all((a, b) in quantised for a in range(m0, m1) for b in range(GROUPS)):
-                    for q in range(4):
-                        queue = nc.scalar if (m1 == TILES and q >= 2) else nc.sync
-                        queue.dma_start(
-                            out=out_2[:, 4 * q:4 * q + 4, m0 * P:m1 * P].rearrange("g r m -> r g m").bitcast(I32),
-                            in_=out_scales[spart][32 * q:32 * q + 4, :, :].bitcast(I32),
-                        )
+        def store_words(part):
+            m0, m1, g0, g1 = part
+            nc.sync.dma_start(
+                out=out_1[g0:g1].rearrange("g p m t -> p g (m t)")[:, :, m0 * P * 4:m1 * P * 4].bitcast(I32),
+                in_=out_words[part][:].bitcast(I32),
+            )
 
-        on_scalar, on_vector = nc.scalar.copy, nc.vector.tensor_copy
-        chan_banks = spread_chan()
-        copy_chan(chan_banks)
+        def store_scales(part):
+            m0, m1 = part
+            for q in range(QUADRANTS):
+                queue = nc.scalar if (m1 == TILES and q >= QUADRANTS // 2) else nc.sync
+                queue.dma_start(
+                    out=out_2[:, 4 * q:4 * q + 4, m0 * P:m1 * P].rearrange("g r m -> r g m").bitcast(I32),
+                    in_=out_scales[part][32 * q:32 * q + 4, :, :].bitcast(I32),
+                )
+
+        def quantise_y(j):
+            for i in range(2):
+                m, g = STEPS[2 * j + i]
+                words_part = [t for t in WORD_PARTS if t[0] <= m < t[1] and t[2] <= g < t[3]][0]
+                scales_part = [t for t in SCALE_PARTS if t[0] <= m < t[1]][0]
+                m0, m1, g0, g1 = words_part
+                n0, n1 = scales_part
+                quantise(out_words[words_part][:, g - g0, (m - m0) * P:(m - m0 + 1) * P],
+                         out_scales[scales_part][:, g, (m - n0) * P:(m - n0 + 1) * P],
+                         y_grouped[j][:, i, :])
+                quantised.add((m, g))
+                if all((mm, gg) in quantised for mm in range(m0, m1) for gg in range(g0, g1)):
+                    store_words(words_part)
+                if all((mm, gg) in quantised for mm in range(n0, n1) for gg in range(GROUPS)):
+                    store_scales(scales_part)
+
+        spread_chan()
         turn_a(0)
         turn_b(0)
         group_a(0)
         group_b(0)
-        group_u(0, PASS)
+        group_u(0, on_vector, 0, PASS)
         quantise_a(0)
         quantise_b(0)
         scale_z(0)
@@ -337,7 +342,8 @@ def tile_frozen_fp4_lowrank_gate_g5_kernel(tc, x, w_words, w_scales, chan, z, la
         corr_matmul(0)
         group_a(1)
         group_b(1)
-        group_u(1, 0)
+        group_u(1, on_scalar, 0, PASS)
+        group_u(2, on_scalar, 0, U2_EARLY)
         quantise_a(1)
         quantise_b(1)
         base_matmul(1)
@@ -351,109 +357,131 @@ def tile_frozen_fp4_lowrank_gate_g5_kernel(tc, x, w_words, w_scales, chan, z, la
         base_matmul(3)
         plus_corr(1)
 
-        for j in range(1, PAIRS - 2):
-            a, b = 2 * j, 2 * j + 1
-            turn_first = [m for m in range(2, TILES) if max(2 * m - 4, 1) == j]
-            turn_second = [m for m in range(2, TILES) if 2 * m - 3 == j]
-            group_first = [m for m in range(2, TILES) if max(2 * m - 4, 1) + 1 == j]
-            group_second = [m for m in range(2, TILES) if 2 * m - 2 == j]
-            quant_first = [m for m in range(2, TILES) if max(2 * m - 4, 1) + 2 == j]
-            quant_second = [m for m in range(2, TILES) if 2 * m - 1 == j]
-            if j == GROUPS - 1:
-                group_a(j)
+        first_late_tile = HEAD_TILES
+        a_slot = {m: max(2 * m - 4, 1) for m in range(first_late_tile, TILES)}
+        b_slot = {m: 2 * m - 3 for m in range(first_late_tile, TILES)}
+        last_slot = SPLIT_PAIR - 1
+
+        def due(turn_slot, j, delay):
+            return [m for m in turn_slot if turn_slot[m] + delay == j]
+
+        for j in range(1, SPLIT_PAIR):
+            s0, s1 = 2 * j, 2 * j + 1
+            new_u = j < GROUPS
+            for m in due(b_slot, j, 1):
+                if m > first_late_tile:
+                    group_b(m)
+            for m in due(a_slot, j, 1):
+                group_a(m, 0, 2 if new_u else 1)
+            if j == last_slot:
+                group_y(j - 4, on_scalar)
             silu(j - 1)
             times_up(j - 1, nc.gpsimd)
-            times_chan(a)
-            if j < GROUPS:
+            times_chan(s0)
+            for m in due(b_slot, j, 2):
+                if m > first_late_tile:
+                    scale_z(m, P // 2, P)
+            if new_u:
                 quantise_u(j)
-                corr_matmul(a)
-                corr_matmul(b)
-            for m in quant_first:
+                corr_matmul(s0)
+                corr_matmul(s1)
+            for m in due(a_slot, j, 2):
                 quantise_a(m)
-            for m in quant_second:
+            for m in due(b_slot, j, 2):
                 quantise_b(m)
-                quantise_z(m)
             if j >= 5:
                 quantise_y(j - 5)
-            if j + 1 < GROUPS:
-                group_u(j + 1, (0, 320)[j - 1])
-            for m in group_first:
-                if j != GROUPS - 1:
-                    group_a(m)
-            for m in group_second:
-                group_b(m)
-            if j >= 4:
+            for m in due(b_slot, j, 2):
+                quantise_z(m)
+            for m in due(b_slot, j, 1):
+                if m > first_late_tile:
+                    scale_z(m, 0, P // 2)
+            if j == 1:
+                group_u(2, on_scalar, U2_EARLY, PASS)
+            if j == 2:
+                group_u(3, on_vector, 0, U3_VECTOR)
+                group_b(first_late_tile)
+            for m in due(a_slot, j, 1):
+                if not new_u:
+                    group_a(m, 1, 2)
+            if 4 <= j < last_slot:
                 group_y(j - 4, on_scalar)
-            base_matmul(a + 2)
-            for m in turn_first:
+            base_matmul(s0 + 2)
+            for m in due(a_slot, j, 0):
                 turn_a(m)
-            for m in turn_second:
+            for m in due(b_slot, j, 0):
                 turn_b(m)
             if j >= 3:
                 turn_y(j - 3)
             if j >= 2:
                 round_y(j - 2, on_scalar)
-            times_chan(b)
-            for m in group_second:
-                scale_z(m)
-            plus_corr(a)
-            plus_corr(b)
+            times_chan(s1)
+            if j == 2:
+                scale_z(first_late_tile)
+                group_u(3, on_scalar, U3_VECTOR, PASS)
+            plus_corr(s0)
+            plus_corr(s1)
             store_y(j - 1)
-            base_matmul(b + 2)
-            if j == PAIRS - 3:
+            base_matmul(s1 + 2)
+            if j == last_slot:
                 turn_y(j - 2)
             if j + 1 >= GROUPS:
-                corr_matmul(a + 2)
-                corr_matmul(b + 2)
+                corr_matmul(s0 + 2)
+                corr_matmul(s1 + 2)
 
-        silu(13)
-        times_up(13, nc.gpsimd)
-        times_chan(28)
-        quantise_y(9)
-        base_matmul(30)
-        round_y(12, on_scalar)
-        group_y(10, on_scalar)
-        group_y(11, on_scalar)
-        times_chan(29)
-        plus_corr(28)
-        plus_corr(29)
-        store_y(13)
-        base_matmul(31)
-        turn_y(12)
-        corr_matmul(30)
-        corr_matmul(31)
-        silu(14, 1, 2)
-        silu(14, 0, 1)
-        times_chan(30)
-        quantise_y(10)
-        quantise_y(11)
-        times_up(14, nc.vector, 1, 2)
-        times_up(14, nc.gpsimd, 0, 1)
-        times_chan(31)
-        store_y(14)
-        round_y(13, on_scalar)
-        turn_y(13)
-        group_y(12, on_scalar)
-        plus_corr(30)
-        plus_corr(31)
-        silu(15, 0, 1)
-        silu(15, 1, 2)
-        quantise_y(12)
-        times_up(15, nc.vector, 0, 1)
-        store_y(15, 0, 1)
-        times_up(15, nc.vector, 1, 2)
-        store_y(15, 1, 2)
-        round_y(14, on_scalar)
-        turn_y(14)
-        group_y(13, on_scalar)
-        round_y(15, on_vector, 0, 1)
-        turn_y(15, 0, 1)
-        round_y(15, on_vector, 1, 2)
-        turn_y(15, 1, 2)
-        group_y(14, on_scalar)
-        quantise_y(13)
-        group_y(15, on_vector, 0, 1)
-        group_y(15, on_scalar, 1, 2)
-        quantise_y(14)
-        quantise_y(15, 0, 1)
-        quantise_y(15, 1, 2)
+        j = SPLIT_PAIR
+        s0, s1 = 2 * j, 2 * j + 1
+        silu(j - 1)
+        times_up(j - 1, nc.gpsimd)
+        times_chan(s0)
+        quantise_y(j - 5)
+        base_matmul(s0 + 2)
+        round_y(j - 2, on_scalar)
+        group_y(j - 4, on_scalar)
+        group_y(j - 3, on_scalar)
+        times_chan(s1)
+        plus_corr(s0)
+        plus_corr(s1)
+        store_y(j - 1)
+        base_matmul(s1 + 2)
+        turn_y(j - 2)
+        corr_matmul(s0 + 2)
+        corr_matmul(s1 + 2)
+
+        j = PAIRS - 1
+        s0, s1 = 2 * j, 2 * j + 1
+        silu(j - 1, 1, 2)
+        silu(j - 1, 0, 1)
+        times_chan(s0)
+        quantise_y(j - 5)
+        quantise_y(j - 4)
+        times_up(j - 1, nc.vector, 1, 2)
+        times_up(j - 1, nc.gpsimd, 0, 1)
+        times_chan(s1)
+        store_y(j - 1, 1, 2)
+        store_y(j - 1, 0, 1)
+        round_y(j - 2, on_scalar)
+        turn_y(j - 2)
+        round_y(j - 1, on_scalar, 1, 2)
+        plus_corr(s0)
+        plus_corr(s1)
+
+        silu(j, 0, 1)
+        silu(j, 1, 2)
+        group_y(j - 3, on_vector)
+        for i in range(2):
+            times_up(j, nc.vector, i, i + 1)
+            store_y(j, i, i + 1)
+        round_y(j - 1, on_scalar, 0, 1)
+        turn_y(j - 1)
+        group_y(j - 2, on_scalar)
+        for i in range(2):
+            round_y(j, on_vector, i, i + 1)
+            turn_y(j, i, i + 1)
+        group_y(j - 1, on_scalar)
+        quantise_y(j - 3)
+        quantise_y(j - 2)
+        group_y(j, on_vector, 0, 1)
+        group_y(j, on_scalar, 1, 2)
+        quantise_y(j - 1)
+        quantise_y(j)

from contextlib import ExitStack

import concourse.mybir as mybir
from concourse.masks import make_identity

M, K, R, N = 1024, 1536, 512, 2048
FLOPS = 2 * M * N * (K + R)

F32 = mybir.dt.float32
BF16 = mybir.dt.bfloat16
I32 = mybir.dt.int32
U32 = mybir.dt.uint32
U8 = mybir.dt.uint8
FP8X4 = mybir.dt.float8_e4m3fn_x4
FP4X4 = mybir.dt.float4_e2m1fn_x4
MULT = mybir.AluOpType.mult
ADD = mybir.AluOpType.add
SILU = mybir.ActivationFunctionType.Silu

P = 128
PASS = 512
QUADRANTS = 4
TILES = M // P
GROUPS = N // PASS
X_PASSES = K // PASS

HEAD_TILES = 2
STEPS = [(m, g) for g in range(GROUPS) for m in range(HEAD_TILES)]
STEPS = STEPS + [(m, g) for m in range(HEAD_TILES, TILES) for g in range(GROUPS)]
PAIRS = len(STEPS) // 2
SPLIT_PAIR = PAIRS - 2

Y_BUFS = 10
U2_EARLY = 192
U3_VECTOR = 320

WORD_PARTS = [(0, 2, 0, 4), (2, 4, 0, 4), (4, 5, 0, 4), (5, 6, 0, 4), (6, 7, 0, 4), (7, 8, 0, 2), (7, 8, 2, 4)]
SCALE_PARTS = [(0, 4), (4, 6), (6, 8)]


def tile_frozen_fp4_lowrank_gate_g5_kernel(tc, x, w_words, w_scales, chan, z, lam, u, up, out_0, out_1, out_2):
    nc = tc.nc
    on_scalar, on_vector = nc.scalar.copy, nc.vector.tensor_copy
    with ExitStack() as ctx:
        sb = ctx.enter_context(tc.tile_pool(name="sb", bufs=1))
        ps = ctx.enter_context(tc.psum_pool(name="ps", bufs=2))
        ctx.enter_context(tc.manual_schedule())

        x_raw, z_raw, up_raw, u_raw, w_codes, w_plane = {}, {}, {}, {}, {}, {}
        bank_a, bank_b, x_grouped_a, x_grouped_b, z_grouped, u_grouped = {}, {}, {}, {}, {}, {}
        act_codes, act_scales, u_codes, u_scales = {}, {}, {}, {}
        base, corr, y, y_sorted, y_bank, y_grouped = {}, {}, {}, {}, {}, {}
        out_words, out_scales, quantised = {}, {}, set()

        def pair_view(tensor, j):
            (m, g), (m_next, g_next) = STEPS[2 * j], STEPS[2 * j + 1]
            if g_next == g:
                return tensor[m * P:(m_next + 1) * P, g * PASS:(g + 1) * PASS].rearrange("(i p) n -> p i n", i=2)
            return tensor[m * P:(m + 1) * P, g * PASS:(g_next + 1) * PASS].rearrange("p (i n) -> p i n", i=2)

        def step_rows(tiles, name, dtype, bufs, j, i0, i1):
            split = j >= SPLIT_PAIR
            key = (j, i0 if split else 0)
            if key not in tiles:
                if split:
                    tiles[key] = sb.tile([P, 1, PASS], dtype, name=name + "_step", bufs=4, align_bytes=64)
                else:
                    tiles[key] = sb.tile([P, 2, PASS], dtype, name=name, bufs=bufs, align_bytes=64)
            return tiles[key][:, i0 - key[1]:i1 - key[1], :]

        def y_rows(j, i0, i1):
            return step_rows(y, "y", F32, Y_BUFS, j, i0, i1)

        def y_sorted_rows(j, i0, i1):
            return step_rows(y_sorted, "y_sorted", BF16, 3, j, i0, i1)

        def load_x(m):
            x_raw[m] = sb.tile([P, K], BF16, name="x_raw", bufs=TILES, align_bytes=64)
            nc.sync.dma_start(out=x_raw[m][:], in_=x[m * P:(m + 1) * P, :])

        def load_z(m):
            z_raw[m] = sb.tile([P, R], BF16, name="z_raw", bufs=TILES, align_bytes=64)
            nc.sync.dma_start(out=z_raw[m][:], in_=z[m * P:(m + 1) * P, :])

        def load_up(j):
            up_raw[j] = sb.tile([P, 2, PASS], BF16, name="up_raw", bufs=PAIRS, align_bytes=64)
            nc.sync.dma_start(out=up_raw[j][:], in_=pair_view(up, j))

        def load_u(g):
            u_raw[g] = sb.tile([P, 4, PASS], BF16, name="u_raw", bufs=GROUPS, align_bytes=64)
            nc.sync.dma_start(out=u_raw[g][:], in_=u[:, g * PASS:(g + 1) * PASS].rearrange("(p t) n -> p t n", t=4))

        def load_w(g):
            w_codes[g] = sb.tile([P, X_PASSES, 2 * PASS], U8, name="w_codes", bufs=GROUPS, align_bytes=64)
            nc.sync.dma_start(
                out=w_codes[g][:].bitcast(I32),
                in_=w_words.rearrange("k p b -> p k b")[:, :, g * 2 * PASS:(g + 1) * 2 * PASS].bitcast(I32),
            )

        def load_w_scales(half):
            cols = slice(half * (N // 2), (half + 1) * (N // 2))
            for q in range(QUADRANTS):
                nc.sync.dma_start(
                    out=w_plane[half][32 * q:32 * q + 4, :, :].bitcast(I32),
                    in_=w_scales[:, 4 * q:4 * q + 4, cols].rearrange("k r n -> r k n").bitcast(I32),
                )

        ident = sb.tile([P, P], F32, name="ident", align_bytes=64)
        make_identity(nc, ident[:])
        for half in range(2):
            w_plane[half] = sb.tile([P, X_PASSES, N // 2], U8, name="w_plane", bufs=2, align_bytes=64)
            nc.vector.memset(w_plane[half][:].bitcast(I32), 0)
        chan_rows = sb.tile([P, N // P], BF16, name="chan_rows", align_bytes=64)
        lam_rows = sb.tile([P, 4], BF16, name="lam_rows", align_bytes=64)
        chan_all = sb.tile([P, N], BF16, name="chan_all", align_bytes=64)

        warm = sb.tile([P, 1], F32, name="warm", align_bytes=64)
        nc.scalar.activation(out=warm[:], in_=ident[:, 0:1], func=SILU)

        nc.sync.dma_start(out=chan_rows[:], in_=chan.rearrange("(p c) -> p c", p=P))
        load_x(0)
        load_u(0)
        load_z(0)
        nc.sync.dma_start(out=lam_rows[:], in_=lam.rearrange("(p t) -> p t", t=4))
        load_x(1)
        load_z(1)
        load_w(0)
        load_w_scales(0)
        load_u(1)
        load_w(1)
        load_u(2)
        load_up(0)
        load_w_scales(1)
        load_w(2)
        load_x(2)
        load_z(2)
        load_u(3)
        load_up(1)
        load_w(3)
        for m in range(3, TILES):
            load_x(m)
            load_z(m)
            load_up(2 * m - 4)
            load_up(2 * m - 3)
        for j in range(2 * TILES - 4, PAIRS):
            load_up(j)

        for part in WORD_PARTS:
            m0, m1, g0, g1 = part
            out_words[part] = sb.tile([P, g1 - g0, (m1 - m0) * P], U32, name="out_words_%d_%d" % (m0, g0), align_bytes=64)
        for part in SCALE_PARTS:
            m0, m1 = part
            out_scales[part] = sb.tile([P, GROUPS, (m1 - m0) * P], U8, name="out_scales_%d" % m0, align_bytes=64)

        def new_bank():
            return ps.tile([P, 4, P], F32, name="turn_bank", bufs=4)

        def turn_pass(bank, quarter, words):
            for h in range(2):
                nc.tensor.transpose(bank[:, quarter + h, :], words[:, h:2 * P:2], ident[:])

        def turn_a(m):
            bank_a[m] = new_bank()
            words = x_raw[m][:].bitcast(F32)
            turn_pass(bank_a[m], 0, words[:, 0:2 * P])
            turn_pass(bank_a[m], 2, words[:, 2 * P:4 * P])

        def turn_b(m):
            bank_b[m] = new_bank()
            turn_pass(bank_b[m], 0, x_raw[m][:].bitcast(F32)[:, 4 * P:6 * P])
            turn_pass(bank_b[m], 2, z_raw[m][:].bitcast(F32))

        def group_a(m, k0=0, k1=2):
            if k0 == 0:
                x_grouped_a[m] = sb.tile([P, 2 * PASS], BF16, name="x_grouped_a", bufs=2, align_bytes=64)
            on_scalar(
                out=x_grouped_a[m][:].bitcast(F32).rearrange("p (k r h) -> p k r h", k=2, h=2)[:, k0:k1],
                in_=bank_a[m][:].rearrange("p (k h) r -> p k r h", h=2)[:, k0:k1],
            )

        def group_b(m):
            x_grouped_b[m] = sb.tile([P, PASS], BF16, name="x_grouped_b", bufs=2, align_bytes=64)
            on_scalar(
                out=x_grouped_b[m][:].bitcast(F32).rearrange("p (r h) -> p r h", h=2),
                in_=bank_b[m][:, 0:2, :].rearrange("p h r -> p r h"),
            )

        def scale_z(m, r0=0, r1=P):
            if r0 == 0:
                z_grouped[m] = sb.tile([P, PASS], BF16, name="z_grouped", bufs=2, align_bytes=64)
            nc.vector.tensor_tensor(
                out=z_grouped[m][:].rearrange("p (r h e) -> p r h e", h=2, e=2)[:, r0:r1],
                in0=lam_rows[:].rearrange("p (h e) -> p h e", e=2).unsqueeze(1).to_broadcast([P, r1 - r0, 2, 2]),
                in1=bank_b[m][:, 2:4, :].bitcast(BF16).rearrange("p h (r e) -> p r h e", e=2)[:, r0:r1],
                op=MULT,
            )

        def quantise(codes, scales, values):
            nc.vector.quantize_mx(out=codes.bitcast(FP8X4), scales=scales, in_=values)

        def quantise_a(m):
            act_codes[m] = sb.tile([P, 4 * P], U32, name="act_codes", bufs=3, align_bytes=64)
            act_scales[m] = sb.tile([P, 4 * P], U8, name="act_scales", bufs=3, align_bytes=64)
            quantise(act_codes[m][:, 0:2 * P], act_scales[m][:, 0:2 * P], x_grouped_a[m][:])

        def quantise_b(m):
            quantise(act_codes[m][:, 2 * P:3 * P], act_scales[m][:, 2 * P:3 * P], x_grouped_b[m][:])

        def quantise_z(m):
            quantise(act_codes[m][:, 3 * P:4 * P], act_scales[m][:, 3 * P:4 * P], z_grouped[m][:])

        def group_u(g, copy, c0, c1):
            if c0 == 0:
                u_grouped[g] = sb.tile([P, 4 * PASS], BF16, name="u_grouped", bufs=3, align_bytes=64)
            columns = u_grouped[g][:].rearrange("p (n t) -> p n t", t=4)[:, c0:c1, :]
            copy(out=columns.rearrange("p (c i) t -> p c t i", i=4),
                 in_=u_raw[g][:, :, c0:c1].rearrange("p t (c i) -> p c t i", i=4))

        def quantise_u(g):
            u_codes[g] = sb.tile([P, PASS], U32, name="u_codes", bufs=GROUPS, align_bytes=64)
            u_scales[g] = sb.tile([P, PASS], U8, name="u_scales", bufs=GROUPS, align_bytes=64)
            quantise(u_codes[g][:], u_scales[g][:], u_grouped[g][:])

        def spread_chan():
            words = chan_rows[:].bitcast(F32)
            spread = chan_all[:].bitcast(F32).rearrange("q (p c) -> q p c", p=P)
            banks = [new_bank(), new_bank()]
            for c in range(8):
                nc.tensor.transpose(banks[c // 4][:, c % 4, :], words[:, c:c + 1].to_broadcast([P, P]), ident[:])
            for i in range(2):
                on_scalar(out=spread[:, :, 4 * i:4 * i + 4], in_=banks[i][:].rearrange("q c p -> q p c"))

        def base_matmul(s):
            m, g = STEPS[s]
            base[s] = ps.tile([P, PASS], F32, name="base")
            for k in range(X_PASSES):
                nc.tensor.matmul_mx(
                    out=base[s][:],
                    lhsT=act_codes[m][:, k * P:(k + 1) * P].bitcast(FP8X4),
                    lhsT_scale=act_scales[m][:, k * P:(k + 1) * P],
                    rhs=w_codes[g][:, k, :].bitcast(FP4X4),
                    rhs_scale=w_plane[g // 2][:, k, (g % 2) * PASS:(g % 2 + 1) * PASS],
                    start=(k == 0),
                    stop=(k == X_PASSES - 1),
                )

        def corr_matmul(s):
            m, g = STEPS[s]
            corr[s] = ps.tile([P, PASS], F32, name="corr")
            nc.tensor.matmul_mx(
                out=corr[s][:],
                lhsT=act_codes[m][:, 3 * P:4 * P].bitcast(FP8X4),
                lhsT_scale=act_scales[m][:, 3 * P:4 * P],
                rhs=u_codes[g][:].bitcast(FP8X4),
                rhs_scale=u_scales[g][:],
                start=True,
                stop=True,
            )

        def times_chan(s):
            g = STEPS[s][1]
            rows = y_rows(s // 2, s % 2, s % 2 + 1)[:, 0, :]
            nc.vector.tensor_tensor(out=rows, in0=chan_all[:, g * PASS:(g + 1) * PASS], in1=base[s][:], op=MULT)

        def plus_corr(s):
            rows = y_rows(s // 2, s % 2, s % 2 + 1)[:, 0, :]
            nc.vector.tensor_tensor(out=rows, in0=rows, in1=corr[s][:], op=ADD)

        def silu(j, i0=0, i1=2):
            nc.scalar.activation(out=y_rows(j, i0, i1), in_=y_rows(j, i0, i1), func=SILU)

        def times_up(j, engine, i0=0, i1=2):
            engine.tensor_tensor(out=y_rows(j, i0, i1), in0=y_rows(j, i0, i1), in1=up_raw[j][:, i0:i1, :], op=MULT)

        def store_y(j, i0=0, i1=2):
            nc.sync.dma_start(out=pair_view(out_0, j)[:, i0:i1, :], in_=y_rows(j, i0, i1))

        def round_y(j, copy, i0=0, i1=2):
            copy(out=y_sorted_rows(j, i0, i1).rearrange("r i (h p e) -> r i h p e", h=2, e=2),
                 in_=y_rows(j, i0, i1).rearrange("r i (p h e) -> r i h p e", h=2, e=2))

        def turn_y(j, i0=0, i1=2):
            bank = new_bank()
            for i in range(i0, i1):
                y_bank[j, i] = bank
                words = y_sorted_rows(j, i, i + 1)[:, 0, :].bitcast(F32)
                for h in range(2):
                    nc.tensor.transpose(bank[:, 2 * i + h, :], words[:, h * P:(h + 1) * P], ident[:])

        def group_y(j, copy, i0=0, i1=2):
            if i0 == 0:
                y_grouped[j] = sb.tile([P, 2, PASS], BF16, name="y_grouped", bufs=4, align_bytes=64)
            copy(out=y_grouped[j][:, i0:i1, :].bitcast(F32).rearrange("p i (r h) -> p i r h", h=2),
                 in_=y_bank[j, i0][:, 2 * i0:2 * i1, :].rearrange("p (i h) r -> p i r h", h=2))

        def store_words(part):
            m0, m1, g0, g1 = part
            nc.sync.dma_start(
                out=out_1[g0:g1].rearrange("g p m t -> p g (m t)")[:, :, m0 * P * 4:m1 * P * 4].bitcast(I32),
                in_=out_words[part][:].bitcast(I32),
            )

        def store_scales(part):
            m0, m1 = part
            for q in range(QUADRANTS):
                queue = nc.scalar if (m1 == TILES and q >= QUADRANTS // 2) else nc.sync
                queue.dma_start(
                    out=out_2[:, 4 * q:4 * q + 4, m0 * P:m1 * P].rearrange("g r m -> r g m").bitcast(I32),
                    in_=out_scales[part][32 * q:32 * q + 4, :, :].bitcast(I32),
                )

        def quantise_y(j):
            for i in range(2):
                m, g = STEPS[2 * j + i]
                words_part = [t for t in WORD_PARTS if t[0] <= m < t[1] and t[2] <= g < t[3]][0]
                scales_part = [t for t in SCALE_PARTS if t[0] <= m < t[1]][0]
                m0, m1, g0, g1 = words_part
                n0, n1 = scales_part
                quantise(out_words[words_part][:, g - g0, (m - m0) * P:(m - m0 + 1) * P],
                         out_scales[scales_part][:, g, (m - n0) * P:(m - n0 + 1) * P],
                         y_grouped[j][:, i, :])
                quantised.add((m, g))
                if all((mm, gg) in quantised for mm in range(m0, m1) for gg in range(g0, g1)):
                    store_words(words_part)
                if all((mm, gg) in quantised for mm in range(n0, n1) for gg in range(GROUPS)):
                    store_scales(scales_part)

        spread_chan()
        turn_a(0)
        turn_b(0)
        group_a(0)
        group_b(0)
        group_u(0, on_vector, 0, PASS)
        quantise_a(0)
        quantise_b(0)
        scale_z(0)
        quantise_u(0)
        quantise_z(0)
        turn_a(1)
        turn_b(1)
        base_matmul(0)
        corr_matmul(0)
        group_a(1)
        group_b(1)
        group_u(1, on_scalar, 0, PASS)
        group_u(2, on_scalar, 0, U2_EARLY)
        quantise_a(1)
        quantise_b(1)
        base_matmul(1)
        scale_z(1)
        times_chan(0)
        quantise_z(1)
        corr_matmul(1)
        base_matmul(2)
        times_chan(1)
        plus_corr(0)
        base_matmul(3)
        plus_corr(1)

        first_late_tile = HEAD_TILES
        a_slot = {m: max(2 * m - 4, 1) for m in range(first_late_tile, TILES)}
        b_slot = {m: 2 * m - 3 for m in range(first_late_tile, TILES)}
        last_slot = SPLIT_PAIR - 1

        def due(turn_slot, j, delay):
            return [m for m in turn_slot if turn_slot[m] + delay == j]

        for j in range(1, SPLIT_PAIR):
            s0, s1 = 2 * j, 2 * j + 1
            new_u = j < GROUPS
            for m in due(b_slot, j, 1):
                if m > first_late_tile:
                    group_b(m)
            for m in due(a_slot, j, 1):
                group_a(m, 0, 2 if new_u else 1)
            if j == last_slot:
                group_y(j - 4, on_scalar)
            silu(j - 1)
            times_up(j - 1, nc.gpsimd)
            times_chan(s0)
            for m in due(b_slot, j, 2):
                if m > first_late_tile:
                    scale_z(m, P // 2, P)
            if new_u:
                quantise_u(j)
                corr_matmul(s0)
                corr_matmul(s1)
            for m in due(a_slot, j, 2):
                quantise_a(m)
            for m in due(b_slot, j, 2):
                quantise_b(m)
            if j >= 5:
                quantise_y(j - 5)
            for m in due(b_slot, j, 2):
                quantise_z(m)
            for m in due(b_slot, j, 1):
                if m > first_late_tile:
                    scale_z(m, 0, P // 2)
            if j == 1:
                group_u(2, on_scalar, U2_EARLY, PASS)
            if j == 2:
                group_u(3, on_vector, 0, U3_VECTOR)
                group_b(first_late_tile)
            for m in due(a_slot, j, 1):
                if not new_u:
                    group_a(m, 1, 2)
            if 4 <= j < last_slot:
                group_y(j - 4, on_scalar)
            base_matmul(s0 + 2)
            for m in due(a_slot, j, 0):
                turn_a(m)
            for m in due(b_slot, j, 0):
                turn_b(m)
            if j >= 3:
                turn_y(j - 3)
            if j >= 2:
                round_y(j - 2, on_scalar)
            times_chan(s1)
            if j == 2:
                scale_z(first_late_tile)
                group_u(3, on_scalar, U3_VECTOR, PASS)
            plus_corr(s0)
            plus_corr(s1)
            store_y(j - 1)
            base_matmul(s1 + 2)
            if j == last_slot:
                turn_y(j - 2)
            if j + 1 >= GROUPS:
                corr_matmul(s0 + 2)
                corr_matmul(s1 + 2)

        j = SPLIT_PAIR
        s0, s1 = 2 * j, 2 * j + 1
        silu(j - 1)
        times_up(j - 1, nc.gpsimd)
        times_chan(s0)
        quantise_y(j - 5)
        base_matmul(s0 + 2)
        round_y(j - 2, on_scalar)
        group_y(j - 4, on_scalar)
        group_y(j - 3, on_scalar)
        times_chan(s1)
        plus_corr(s0)
        plus_corr(s1)
        store_y(j - 1)
        base_matmul(s1 + 2)
        turn_y(j - 2)
        corr_matmul(s0 + 2)
        corr_matmul(s1 + 2)

        j = PAIRS - 1
        s0, s1 = 2 * j, 2 * j + 1
        silu(j - 1, 1, 2)
        silu(j - 1, 0, 1)
        times_chan(s0)
        quantise_y(j - 5)
        quantise_y(j - 4)
        times_up(j - 1, nc.vector, 1, 2)
        times_up(j - 1, nc.gpsimd, 0, 1)
        times_chan(s1)
        store_y(j - 1, 1, 2)
        store_y(j - 1, 0, 1)
        round_y(j - 2, on_scalar)
        turn_y(j - 2)
        round_y(j - 1, on_scalar, 1, 2)
        plus_corr(s0)
        plus_corr(s1)

        silu(j, 0, 1)
        silu(j, 1, 2)
        group_y(j - 3, on_vector)
        for i in range(2):
            times_up(j, nc.vector, i, i + 1)
            store_y(j, i, i + 1)
        round_y(j - 1, on_scalar, 0, 1)
        turn_y(j - 1)
        group_y(j - 2, on_scalar)
        for i in range(2):
            round_y(j, on_vector, i, i + 1)
            turn_y(j, i, i + 1)
        group_y(j - 1, on_scalar)
        quantise_y(j - 3)
        quantise_y(j - 2)
        group_y(j, on_vector, 0, 1)
        group_y(j, on_scalar, 1, 2)
        quantise_y(j - 1)
        quantise_y(j)
